import numpy as np
import ml_dtypes


def mxq(x, axis, fmt="e4m3"):
    dtype, down = {"e4m3": (ml_dtypes.float8_e4m3fn, 7), "e5m2": (ml_dtypes.float8_e5m2, 14)}[fmt]
    v = np.moveaxis(np.asarray(x, np.float32).astype(ml_dtypes.bfloat16).astype(np.float64), axis, -1)
    blocks = v.reshape(v.shape[:-1] + (-1, 32))
    amax = np.abs(blocks).max(-1, keepdims=True)
    byte = np.maximum(np.where(amax > 0, np.frexp(amax)[1] - 1 + 127, 0) - down, 1)
    scale = np.exp2(byte - 127.0)
    codes = (blocks / scale).astype(np.float32).astype(dtype).astype(np.float64)
    return np.moveaxis((codes * scale).reshape(v.shape), -1, axis)


WIDE = False


def mx_kscale(k):
    if not WIDE:
        return np.ones(k)
    levels = np.array([18, -18])
    if k % 512:
        return np.exp2(np.random.permutation(np.resize(levels, k // 32))).repeat(32)
    a = np.empty((k // 512, 16))
    for p in range(k // 512):
        a[p, :8] = np.random.permutation(np.resize(levels, 8))
        for g in range(8):
            far = levels[np.abs(levels - a[p, g]) >= 10]
            a[p, g + 8] = far[np.random.randint(len(far))]
    return np.exp2(a.ravel()).repeat(32)


def f64(x):
    return np.asarray(x).astype(np.float64)


def striped(idx):
    return np.tile(np.asarray(idx).reshape(-1, 16).T, (8, 1)).astype(np.uint16)


def unstriped(offs):
    return offs[:16].T.reshape(-1).astype(np.int64)

def planes(y):
    n, m = y.shape
    v = y.astype(np.float32).astype(ml_dtypes.bfloat16).astype(np.float64).reshape(n // 32, 32, m)
    top = np.abs(v).max(1)
    byte = np.clip(np.where(top > 0, np.frexp(top)[1] - 1 + 127 - 7, 1), 1, 254)
    codes = (v * np.exp2(127.0 - byte)[:, None, :]).reshape(n, m).astype(np.float32).astype(ml_dtypes.float8_e4m3fn).view(np.uint8)
    words = codes.reshape(n // 512, 128, 4, m).transpose(0, 1, 3, 2)
    return np.ascontiguousarray(words), np.ascontiguousarray(byte.astype(np.uint8).reshape(n // 512, 16, m))


def setup_inputs():
    n = np.random.standard_normal
    uni = np.random.uniform
    idx = np.random.permutation(2048)[:512]
    f_f = mx_kscale(512)
    f_r = mx_kscale(512)
    return {
        "qT": (n((512, 512)) * f_r[None, :]).astype(np.float32),
        "G": (n((512, 512)) / np.sqrt(512) / f_r[:, None]).astype(np.float32),
        "wk": (n((512, 512)) / np.sqrt(512) * f_f[None, :]).astype(np.float32),
        "ts": np.tile(uni(0.75, 1.3, 2048), (128, 1)).astype(np.float32),
        "cf": (uni(0.75, 1.3, (512, 1)) / f_f[:, None]).astype(np.float32),
        "offs": striped(idx),
    }


def reference(qT, G, wk, ts, cf, offs):
    idx = unstriped(offs)
    ts_i = f64(ts)[:1][:, idx]
    b = mxq(f64(qT), 1, "e4m3") @ mxq(f64(G), 0, "e5m2")
    dk = f64(cf) * ts_i * b
    dc = mxq(f64(wk), 1, "e4m3") @ mxq(dk, 0, "e5m2")
    out_0 = np.zeros((512, 2048))
    out_0[:, idx] = dc
    return (out_0,) + planes(out_0)

@@ -1,0 +1,217 @@
+from contextlib import ExitStack
+
+import concourse.mybir as mybir
+from concourse.masks import make_identity
+
+F32 = mybir.dt.float32
+BF16 = mybir.dt.bfloat16
+I32 = mybir.dt.int32
+U32 = mybir.dt.uint32
+U16 = mybir.dt.uint16
+U8 = mybir.dt.uint8
+E4M3 = mybir.dt.float8_e4m3fn_x4
+E5M2 = mybir.dt.float8_e5m2_x4
+MULT = mybir.AluOpType.mult
+
+P = 128
+LANES = 4
+K = 512
+SLOTS = 512
+TOKENS = 2048
+CHUNK = 512
+CHUNKS = TOKENS // CHUNK
+G_HALF = SLOTS // 2
+G_VECTOR_COLS = 168
+DK_VECTOR_COLS = 344
+
+FLOPS = 2 * 2 * 512 * 512 * 512
+
+
+def tile_attend_gmla_c_pl_kernel(tc, qT, G, wk, ts, cf, offs, out_0, out_1, out_2):
+    nc = tc.nc
+    with ExitStack() as ctx:
+        keep = ctx.enter_context(tc.tile_pool(name="keep", bufs=1))
+        psum = ctx.enter_context(tc.psum_pool(name="psum", bufs=1))
+        turn = ctx.enter_context(tc.psum_pool(name="turn", bufs=3))
+
+        offsets = keep.tile([P, SLOTS // 16], U16, name="offsets")
+        nc.sync.dma_start(offsets[:], offs)
+
+        ts_window = keep.tile([P, TOKENS], F32, name="ts_window")
+        warm = keep.tile([P, 8], F32, name="warm")
+        warmed = keep.tile([P, 8], F32, name="warmed")
+        nc.vector.memset(warm[:], 0.0)
+        nc.scalar.copy(warmed[:], warm[:])
+        nc.vector.memset(ts_window[:].bitcast(I32), 0)
+        nc.scalar.dma_start(ts_window[0:1, :], ts[0:1, :])
+        cf_cols = keep.tile([P, LANES], F32, name="cf_cols")
+        nc.scalar.dma_start(cf_cols[:], cf.rearrange("(p t) o -> p (t o)", t=LANES))
+
+        q_rows = qT.rearrange("(m t) r -> m t r", t=LANES)
+        w_rows = wk.rearrange("(m t) f -> m t f", t=LANES)
+        g_rows = G.rearrange("(p j) i -> p j i", j=LANES)
+        q_raw = [keep.tile([P, K], F32, name="q_raw%d" % t) for t in range(LANES)]
+        w_raw = [keep.tile([P, K], F32, name="w_raw%d" % t) for t in range(LANES)]
+        g_raw = [keep.tile([P, LANES, G_HALF], F32, name="g_raw%d" % h) for h in range(2)]
+        for t in (0, 1):
+            nc.sync.dma_start(q_raw[t][:], q_rows[:, t, :])
+        for h in range(2):
+            nc.sync.dma_start(g_raw[h][:], g_rows[:, :, h * G_HALF : (h + 1) * G_HALF])
+        for t in (2, 3):
+            nc.sync.dma_start(q_raw[t][:], q_rows[:, t, :])
+        for t in range(LANES):
+            nc.sync.dma_start(w_raw[t][:], w_rows[:, t, :])
+
+        ident = keep.tile([P, P], F32, name="ident")
+        make_identity(nc, ident[:])
+
+        windows = [keep.tile([P, TOKENS], F32, name="window%d" % w) for w in range(2)]
+        for w in range(2):
+            nc.vector.memset(windows[w][:].bitcast(I32), 0)
+
+        def stationary(raw, name):
+            paired = keep.tile([P, 2, P, 2], BF16, name=name + "_paired", align_bytes=64)
+            nc.scalar.copy(paired[:], raw[:].rearrange("m (p u e) -> m u p e", u=2, e=2))
+            words = paired[:].rearrange("m u p e -> m (u p e)").bitcast(F32)
+            turned = turn.tile([P, 2, P], F32, name="turned")
+            for u in range(2):
+                nc.tensor.transpose(turned[:, u, :], words[:, u * P : (u + 1) * P], ident[:])
+            grouped = keep.tile([P, K], BF16, name=name + "_grouped", align_bytes=64)
+            nc.scalar.copy(
+                grouped[:].bitcast(F32).rearrange("p (m u) -> p m u", u=2),
+                turned[:].rearrange("p u m -> p m u"),
+            )
+            codes = keep.tile([P, P], U32, name=name + "_codes", align_bytes=64)
+            scales = keep.tile([P, P], U8, name=name + "_scales", align_bytes=64)
+            nc.vector.quantize_mx(out=codes[:].bitcast(E4M3), scales=scales[:], in_=grouped[:])
+            return codes, scales
+
+        def interleave(dst, src, vector_cols):
+            cols = dst.shape[1]
+            dst4 = dst[:].rearrange("p (c i) t -> p c t i", i=4)
+            src4 = src[:].rearrange("p t (c i) -> p c t i", i=4)
+            cut = vector_cols // 4
+            nc.vector.tensor_copy(dst4[:, :cut], src4[:, :cut])
+            nc.scalar.copy(dst4[:, cut : cols // 4], src4[:, cut : cols // 4])
+
+        q_ops = {}
+        for t in (0, 1):
+            q_ops[t] = stationary(q_raw[t], "q%d" % t)
+
+        ts_row = keep.tile([P, SLOTS], F32, name="ts_row")
+        nc.vector.tensor_copy(ts_row[:], ts_window[:].indirect(offsets[:]))
+        ts_turned = turn.tile([P, LANES, P], F32, name="turned")
+        for s in range(SLOTS // P):
+            nc.tensor.transpose(ts_turned[:, s, :], ts_row[:, s * P : (s + 1) * P], ident[:])
+        ts_cols = keep.tile([P, SLOTS // P], F32, name="ts_cols")
+        nc.vector.tensor_copy(ts_cols[:], ts_turned[:, :, 0])
+        ts_bank = psum.tile([P, SLOTS], F32, name="ts_bank")
+        for s in range(SLOTS // P):
+            nc.tensor.transpose(ts_bank[:, s * P : (s + 1) * P], ts_cols[:, s : s + 1].to_broadcast([P, P]), ident[:])
+        ts_all = keep.tile([P, SLOTS], F32, name="ts_all")
+        nc.scalar.copy(ts_all[:], ts_bank[:])
+
+        g_codes = keep.tile([P, SLOTS], U32, name="g_codes", align_bytes=64)
+        g_scales = keep.tile([P, SLOTS], U8, name="g_scales", align_bytes=64)
+        for h in range(2):
+            g_grouped = keep.tile([P, G_HALF, LANES], BF16, name="g_grouped%d" % h, align_bytes=64)
+            interleave(g_grouped, g_raw[h], G_VECTOR_COLS)
+            cols = slice(h * G_HALF, (h + 1) * G_HALF)
+            nc.vector.quantize_mx(
+                out=g_codes[:, cols].bitcast(E5M2), scales=g_scales[:, cols],
+                in_=g_grouped[:].rearrange("p c t -> p (c t)"))
+
+        for t in (2, 3):
+            q_ops[t] = stationary(q_raw[t], "q%d" % t)
+
+        dk_rows = keep.tile([P, LANES, SLOTS], BF16, name="dk_rows", align_bytes=64)
+        for t in range(LANES):
+            acc = psum.tile([P, SLOTS], F32, name="acc%d" % t)
+            nc.tensor.matmul_mx(
+                out=acc[:], lhsT=q_ops[t][0][:].bitcast(E4M3), lhsT_scale=q_ops[t][1][:],
+                rhs=g_codes[:].bitcast(E5M2), rhs_scale=g_scales[:], start=True, stop=True)
+            nc.vector.scalar_tensor_tensor(
+                out=dk_rows[:, t, :], in0=acc[:], scalar=cf_cols[:, t : t + 1], in1=ts_all[:], op0=MULT, op1=MULT)
+
+        w_ops = {}
+        for t in (0, 1):
+            w_ops[t] = stationary(w_raw[t], "w%d" % t)
+
+        dk_grouped = keep.tile([P, SLOTS, LANES], BF16, name="dk_grouped", tag="late", align_bytes=64)
+        interleave(dk_grouped, dk_rows, DK_VECTOR_COLS)
+        dk_codes = keep.tile([P, SLOTS], U32, name="dk_codes", align_bytes=64)
+        dk_scales = keep.tile([P, SLOTS], U8, name="dk_scales", align_bytes=64)
+        nc.vector.quantize_mx(
+            out=dk_codes[:].bitcast(E5M2), scales=dk_scales[:], in_=dk_grouped[:].rearrange("p c t -> p (c t)"))
+
+        late_window = keep.tile([P, TOKENS], F32, name="window2", tag="late", align_bytes=64)
+        nc.vector.memset(late_window[:].bitcast(I32), 0)
+        windows.append(late_window)
+
+        dc = []
+
+        def product(t):
+            acc = psum.tile([P, SLOTS], F32, name="acc%d" % t)
+            nc.tensor.matmul_mx(
+                out=acc[:], lhsT=w_ops[t][0][:].bitcast(E4M3), lhsT_scale=w_ops[t][1][:],
+                rhs=dk_codes[:].bitcast(E5M2), rhs_scale=dk_scales[:], start=True, stop=True)
+            dc_t = keep.tile([P, SLOTS], F32, name="dc%d" % t)
+            nc.scalar.copy(dc_t[:], acc[:])
+            dc.append(dc_t)
+
+        for t in (0, 1):
+            product(t)
+        for t in (2, 3):
+            w_ops[t] = stationary(w_raw[t], "w%d" % t)
+        for t in (2, 3):
+            product(t)
+
+        out_rows = out_0.rearrange("(p t) c -> p t c", t=LANES)
+        pairs = [keep.tile([P, 2, CHUNK, 2], BF16, name="pairs%d" % c, align_bytes=64) for c in range(CHUNKS)]
+
+        def round_lane(engine_copy, t, c):
+            engine_copy(pairs[c][:, t // 2, :, t % 2], windows[t % 3][:, c * CHUNK : (c + 1) * CHUNK])
+
+        for t in range(LANES):
+            window = windows[t % 3]
+            nc.vector.tensor_copy(window[:].indirect(offsets[:]), dc[t][:])
+            nc.sync.dma_start(out_rows[:, t, :], window[:])
+            if t < LANES - 1:
+                for c in range(CHUNKS):
+                    if (t, c) == (LANES - 2, 0):
+                        nc.scalar.copy(pairs[0][:, 1], window[:, :CHUNK].unsqueeze(2).to_broadcast([P, CHUNK, 2]))
+                    else:
+                        round_lane(nc.scalar.copy, t, c)
+
+        last = LANES - 1
+        words_out = out_1[0].rearrange("p c l -> p (c l)").bitcast(I32)
+        y_scales = keep.tile([P, TOKENS], U8, name="y_scales", align_bytes=64)
+        y_grouped = [keep.tile([P, CHUNK * LANES], BF16, name="y_grouped%d" % c, align_bytes=64) for c in range(CHUNKS)]
+
+        def merge(engine_copy, c):
+            engine_copy(
+                y_grouped[c][:].bitcast(F32).rearrange("p (c u) -> p c u", u=2),
+                pairs[c][:].rearrange("p u c e -> p (u c e)").bitcast(F32).rearrange("p (u c) -> p c u", u=2),
+            )
+
+        def quantise(c):
+            cols = slice(c * CHUNK, (c + 1) * CHUNK)
+            y_codes = keep.tile([P, CHUNK], U32, name="y_codes%d" % c, align_bytes=64)
+            nc.vector.quantize_mx(out=y_codes[:].bitcast(E4M3), scales=y_scales[:, cols], in_=y_grouped[c][:])
+            nc.sync.dma_start(words_out[:, cols], y_codes[:].bitcast(I32))
+
+        round_lane(nc.vector.tensor_copy, last, 0)
+        for c in range(1, CHUNKS):
+            round_lane(nc.scalar.copy, last, c)
+        merge(nc.scalar.copy, CHUNKS - 1)
+        merge(nc.vector.tensor_copy, 0)
+        merge(nc.vector.tensor_copy, 1)
+        quantise(0)
+        merge(nc.vector.tensor_copy, 2)
+        for c in range(1, CHUNKS):
+            quantise(c)
+        for quad in range(4):
+            queue = nc.sync if quad % 2 == 0 else nc.scalar
+            queue.dma_start(
+                out_2[0, 4 * quad : 4 * quad + 4, :].bitcast(I32),
+                y_scales[32 * quad : 32 * quad + 4, :].bitcast(I32))

@@ -22,7 +22,7 @@ CHUNK = 512
 CHUNKS = TOKENS // CHUNK
 G_HALF = SLOTS // 2
 G_VECTOR_COLS = 168
-DK_VECTOR_COLS = 344
+DK_VECTOR_COLS = 512
 
 FLOPS = 2 * 2 * 512 * 512 * 512
 
@@ -43,7 +43,6 @@ def tile_attend_gmla_c_pl_kernel(tc, qT, G, wk, ts, cf, offs, out_0, out_1, out_
         nc.vector.memset(warm[:], 0.0)
         nc.scalar.copy(warmed[:], warm[:])
         nc.vector.memset(ts_window[:].bitcast(I32), 0)
-        nc.scalar.dma_start(ts_window[0:1, :], ts[0:1, :])
         cf_cols = keep.tile([P, LANES], F32, name="cf_cols")
         nc.scalar.dma_start(cf_cols[:], cf.rearrange("(p t) o -> p (t o)", t=LANES))
 
@@ -53,10 +52,12 @@ def tile_attend_gmla_c_pl_kernel(tc, qT, G, wk, ts, cf, offs, out_0, out_1, out_
         q_raw = [keep.tile([P, K], F32, name="q_raw%d" % t) for t in range(LANES)]
         w_raw = [keep.tile([P, K], F32, name="w_raw%d" % t) for t in range(LANES)]
         g_raw = [keep.tile([P, LANES, G_HALF], F32, name="g_raw%d" % h) for h in range(2)]
-        for t in (0, 1):
-            nc.sync.dma_start(q_raw[t][:], q_rows[:, t, :])
-        for h in range(2):
-            nc.sync.dma_start(g_raw[h][:], g_rows[:, :, h * G_HALF : (h + 1) * G_HALF])
+        nc.sync.dma_start(q_raw[0][:], q_rows[:, 0, :])
+        nc.sync.dma_start(ts_window[0:1, :], ts[0:1, :])
+        nc.sync.dma_start(q_raw[1][:], q_rows[:, 1, :])
+        for j in range(LANES):
+            nc.sync.dma_start(g_raw[0][:, j, :], g_rows[:, j, :G_HALF])
+        nc.sync.dma_start(g_raw[1][:], g_rows[:, :, G_HALF:])
         for t in (2, 3):
             nc.sync.dma_start(q_raw[t][:], q_rows[:, t, :])
         for t in range(LANES):
@@ -66,8 +67,8 @@ def tile_attend_gmla_c_pl_kernel(tc, qT, G, wk, ts, cf, offs, out_0, out_1, out_
         make_identity(nc, ident[:])
 
         windows = [keep.tile([P, TOKENS], F32, name="window%d" % w) for w in range(2)]
-        for w in range(2):
-            nc.vector.memset(windows[w][:].bitcast(I32), 0)
+        nc.vector.memset(windows[0][:].bitcast(I32), 0)
+        nc.gpsimd.memset(windows[1][:].bitcast(I32), 0)
 
         def stationary(raw, name):
             paired = keep.tile([P, 2, P, 2], BF16, name=name + "_paired", align_bytes=64)
@@ -91,8 +92,10 @@ def tile_attend_gmla_c_pl_kernel(tc, qT, G, wk, ts, cf, offs, out_0, out_1, out_
             dst4 = dst[:].rearrange("p (c i) t -> p c t i", i=4)
             src4 = src[:].rearrange("p t (c i) -> p c t i", i=4)
             cut = vector_cols // 4
-            nc.vector.tensor_copy(dst4[:, :cut], src4[:, :cut])
-            nc.scalar.copy(dst4[:, cut : cols // 4], src4[:, cut : cols // 4])
+            if cut > 0:
+                nc.vector.tensor_copy(dst4[:, :cut], src4[:, :cut])
+            if cut < cols // 4:
+                nc.scalar.copy(dst4[:, cut : cols // 4], src4[:, cut : cols // 4])
 
         q_ops = {}
         for t in (0, 1):
@@ -108,18 +111,19 @@ def tile_attend_gmla_c_pl_kernel(tc, qT, G, wk, ts, cf, offs, out_0, out_1, out_
         ts_bank = psum.tile([P, SLOTS], F32, name="ts_bank")
         for s in range(SLOTS // P):
             nc.tensor.transpose(ts_bank[:, s * P : (s + 1) * P], ts_cols[:, s : s + 1].to_broadcast([P, P]), ident[:])
-        ts_all = keep.tile([P, SLOTS], F32, name="ts_all")
-        nc.scalar.copy(ts_all[:], ts_bank[:])
 
         g_codes = keep.tile([P, SLOTS], U32, name="g_codes", align_bytes=64)
         g_scales = keep.tile([P, SLOTS], U8, name="g_scales", align_bytes=64)
         for h in range(2):
             g_grouped = keep.tile([P, G_HALF, LANES], BF16, name="g_grouped%d" % h, align_bytes=64)
-            interleave(g_grouped, g_raw[h], G_VECTOR_COLS)
+            interleave(g_grouped, g_raw[h], G_HALF * h)
             cols = slice(h * G_HALF, (h + 1) * G_HALF)
             nc.vector.quantize_mx(
                 out=g_codes[:, cols].bitcast(E5M2), scales=g_scales[:, cols],
                 in_=g_grouped[:].rearrange("p c t -> p (c t)"))
+
+        ts_all = keep.tile([P, SLOTS], F32, name="ts_all")
+        nc.vector.tensor_copy(ts_all[:], ts_bank[:])
 
         for t in (2, 3):
             q_ops[t] = stationary(q_raw[t], "q%d" % t)

@@ -17,12 +17,12 @@ P = 128
 LANES = 4
 K = 512
 SLOTS = 512
+TILES = SLOTS // P
 TOKENS = 2048
 CHUNK = 512
 CHUNKS = TOKENS // CHUNK
 G_HALF = SLOTS // 2
-G_VECTOR_COLS = 168
-DK_VECTOR_COLS = 512
+TS_ROW = P - 1
 
 FLOPS = 2 * 2 * 512 * 512 * 512
 
@@ -32,143 +32,157 @@ def tile_attend_gmla_c_pl_kernel(tc, qT, G, wk, ts, cf, offs, out_0, out_1, out_
     with ExitStack() as ctx:
         keep = ctx.enter_context(tc.tile_pool(name="keep", bufs=1))
         psum = ctx.enter_context(tc.psum_pool(name="psum", bufs=1))
-        turn = ctx.enter_context(tc.psum_pool(name="turn", bufs=3))
+        turn = ctx.enter_context(tc.psum_pool(name="turn", bufs=4))
 
-        offsets = keep.tile([P, SLOTS // 16], U16, name="offsets")
-        nc.sync.dma_start(offsets[:], offs)
-
-        ts_window = keep.tile([P, TOKENS], F32, name="ts_window")
-        warm = keep.tile([P, 8], F32, name="warm")
-        warmed = keep.tile([P, 8], F32, name="warmed")
-        nc.vector.memset(warm[:], 0.0)
-        nc.scalar.copy(warmed[:], warm[:])
-        nc.vector.memset(ts_window[:].bitcast(I32), 0)
-        cf_cols = keep.tile([P, LANES], F32, name="cf_cols")
-        nc.scalar.dma_start(cf_cols[:], cf.rearrange("(p t) o -> p (t o)", t=LANES))
-
-        q_rows = qT.rearrange("(m t) r -> m t r", t=LANES)
+        q_rows = qT.rearrange("(h m u) r -> u h m r", h=2, u=2)
         w_rows = wk.rearrange("(m t) f -> m t f", t=LANES)
         g_rows = G.rearrange("(p j) i -> p j i", j=LANES)
         q_raw = [keep.tile([P, K], F32, name="q_raw%d" % t) for t in range(LANES)]
         w_raw = [keep.tile([P, K], F32, name="w_raw%d" % t) for t in range(LANES)]
         g_raw = [keep.tile([P, LANES, G_HALF], F32, name="g_raw%d" % h) for h in range(2)]
-        nc.sync.dma_start(q_raw[0][:], q_rows[:, 0, :])
-        nc.sync.dma_start(ts_window[0:1, :], ts[0:1, :])
-        nc.sync.dma_start(q_raw[1][:], q_rows[:, 1, :])
-        for j in range(LANES):
-            nc.sync.dma_start(g_raw[0][:, j, :], g_rows[:, j, :G_HALF])
-        nc.sync.dma_start(g_raw[1][:], g_rows[:, :, G_HALF:])
-        for t in (2, 3):
-            nc.sync.dma_start(q_raw[t][:], q_rows[:, t, :])
+        offsets = keep.tile([P, SLOTS // 16], U16, name="offsets")
+        ts_window = keep.tile([P, TOKENS], F32, name="ts_window")
+        cf_cols = keep.tile([P, LANES], F32, name="cf_cols")
+
+        nc.scalar.dma_start(ts_window[TS_ROW:P, :], ts[0:1, :])
+        nc.scalar.dma_start(cf_cols[:], cf.rearrange("(p t) o -> p (t o)", t=LANES))
+        nc.sync.dma_start(q_raw[0][:], q_rows[0, 0])
+        nc.sync.dma_start(offsets[:], offs)
+        for t in range(1, LANES):
+            nc.sync.dma_start(q_raw[t][:], q_rows[t // 2, t % 2])
+        for h in range(2):
+            nc.sync.dma_start(g_raw[h][:], g_rows[:, :, h * G_HALF : (h + 1) * G_HALF])
         for t in range(LANES):
             nc.sync.dma_start(w_raw[t][:], w_rows[:, t, :])
 
         ident = keep.tile([P, P], F32, name="ident")
         make_identity(nc, ident[:])
 
-        windows = [keep.tile([P, TOKENS], F32, name="window%d" % w) for w in range(2)]
-        nc.vector.memset(windows[0][:].bitcast(I32), 0)
-        nc.gpsimd.memset(windows[1][:].bitcast(I32), 0)
+        nc.vector.memset(ts_window[0:TS_ROW, :].bitcast(I32), 0)
+        windows = [keep.tile([P, TOKENS], F32, name="window0")]
+        nc.gpsimd.memset(windows[0][:].bitcast(I32), 0)
 
-        def stationary(raw, name):
-            paired = keep.tile([P, 2, P, 2], BF16, name=name + "_paired", align_bytes=64)
-            nc.scalar.copy(paired[:], raw[:].rearrange("m (p u e) -> m u p e", u=2, e=2))
-            words = paired[:].rearrange("m u p e -> m (u p e)").bitcast(F32)
+        def turn_words(paired, grouped):
+            words = paired.bitcast(F32)
             turned = turn.tile([P, 2, P], F32, name="turned")
             for u in range(2):
                 nc.tensor.transpose(turned[:, u, :], words[:, u * P : (u + 1) * P], ident[:])
-            grouped = keep.tile([P, K], BF16, name=name + "_grouped", align_bytes=64)
             nc.scalar.copy(
-                grouped[:].bitcast(F32).rearrange("p (m u) -> p m u", u=2),
+                grouped.bitcast(F32).rearrange("p (m u) -> p m u", u=2),
                 turned[:].rearrange("p u m -> p m u"),
             )
-            codes = keep.tile([P, P], U32, name=name + "_codes", align_bytes=64)
-            scales = keep.tile([P, P], U8, name=name + "_scales", align_bytes=64)
-            nc.vector.quantize_mx(out=codes[:].bitcast(E4M3), scales=scales[:], in_=grouped[:])
-            return codes, scales
 
-        def interleave(dst, src, vector_cols):
-            cols = dst.shape[1]
-            dst4 = dst[:].rearrange("p (c i) t -> p c t i", i=4)
-            src4 = src[:].rearrange("p t (c i) -> p c t i", i=4)
-            cut = vector_cols // 4
-            if cut > 0:
-                nc.vector.tensor_copy(dst4[:, :cut], src4[:, :cut])
-            if cut < cols // 4:
-                nc.scalar.copy(dst4[:, cut : cols // 4], src4[:, cut : cols // 4])
+        def stage(name, tag):
+            return keep.tile([P, K], BF16, name=name, tag=tag, align_bytes=64)
 
-        q_ops = {}
-        for t in (0, 1):
-            q_ops[t] = stationary(q_raw[t], "q%d" % t)
+        def round_pairs(round_copy, raw, order, paired):
+            round_copy(paired[:].rearrange("m (u p e) -> m u p e", u=2, e=2), raw[:].rearrange(order, u=2, e=2))
 
         ts_row = keep.tile([P, SLOTS], F32, name="ts_row")
         nc.vector.tensor_copy(ts_row[:], ts_window[:].indirect(offsets[:]))
-        ts_turned = turn.tile([P, LANES, P], F32, name="turned")
-        for s in range(SLOTS // P):
+
+        q_codes = keep.tile([P, K], U32, name="q_codes", align_bytes=64)
+        q_scales = keep.tile([P, K], U8, name="q_scales", align_bytes=64)
+        for t in range(LANES):
+            cols = slice(t * P, (t + 1) * P)
+            round_copy = nc.scalar.copy if t % 2 == 0 else nc.vector.tensor_copy
+            paired = stage("q_paired%d" % t, "q_paired%d" % t)
+            round_pairs(round_copy, q_raw[t], "m (p u e) -> m u p e", paired)
+            grouped = stage("q_grouped%d" % t, "q_grouped%d" % t)
+            turn_words(paired[:], grouped[:])
+            nc.vector.quantize_mx(out=q_codes[:, cols].bitcast(E4M3), scales=q_scales[:, cols], in_=grouped[:])
+
+        ts_turned = turn.tile([P, TILES, P], F32, name="turned")
+        for s in range(TILES):
             nc.tensor.transpose(ts_turned[:, s, :], ts_row[:, s * P : (s + 1) * P], ident[:])
-        ts_cols = keep.tile([P, SLOTS // P], F32, name="ts_cols")
-        nc.vector.tensor_copy(ts_cols[:], ts_turned[:, :, 0])
-        ts_bank = psum.tile([P, SLOTS], F32, name="ts_bank")
-        for s in range(SLOTS // P):
-            nc.tensor.transpose(ts_bank[:, s * P : (s + 1) * P], ts_cols[:, s : s + 1].to_broadcast([P, P]), ident[:])
+        ts_cols = keep.tile([P, TILES], F32, name="ts_cols")
+        nc.vector.tensor_copy(ts_cols[:], ts_turned[:, :, TS_ROW])
+
+        cf_turned = turn.tile([P, LANES, P], F32, name="turned")
+        for t in range(LANES):
+            nc.tensor.transpose(cf_turned[:, t, :], cf_cols[:, t : t + 1].to_broadcast([P, P]), ident[:])
+        cf_all = keep.tile([P, K], F32, name="cf_all")
+        nc.vector.tensor_copy(
+            cf_all[:].rearrange("i (u p e) -> i u p e", u=2, e=2),
+            cf_turned[:].rearrange("i (e u) p -> i u p e", u=2),
+        )
 
         g_codes = keep.tile([P, SLOTS], U32, name="g_codes", align_bytes=64)
         g_scales = keep.tile([P, SLOTS], U8, name="g_scales", align_bytes=64)
-        for h in range(2):
-            g_grouped = keep.tile([P, G_HALF, LANES], BF16, name="g_grouped%d" % h, align_bytes=64)
-            interleave(g_grouped, g_raw[h], G_HALF * h)
-            cols = slice(h * G_HALF, (h + 1) * G_HALF)
-            nc.vector.quantize_mx(
-                out=g_codes[:, cols].bitcast(E5M2), scales=g_scales[:, cols],
-                in_=g_grouped[:].rearrange("p c t -> p (c t)"))
-
-        ts_all = keep.tile([P, SLOTS], F32, name="ts_all")
-        nc.vector.tensor_copy(ts_all[:], ts_bank[:])
-
-        for t in (2, 3):
-            q_ops[t] = stationary(q_raw[t], "q%d" % t)
-
-        dk_rows = keep.tile([P, LANES, SLOTS], BF16, name="dk_rows", align_bytes=64)
-        for t in range(LANES):
-            acc = psum.tile([P, SLOTS], F32, name="acc%d" % t)
-            nc.tensor.matmul_mx(
-                out=acc[:], lhsT=q_ops[t][0][:].bitcast(E4M3), lhsT_scale=q_ops[t][1][:],
-                rhs=g_codes[:].bitcast(E5M2), rhs_scale=g_scales[:], start=True, stop=True)
-            nc.vector.scalar_tensor_tensor(
-                out=dk_rows[:, t, :], in0=acc[:], scalar=cf_cols[:, t : t + 1], in1=ts_all[:], op0=MULT, op1=MULT)
-
-        w_ops = {}
-        for t in (0, 1):
-            w_ops[t] = stationary(w_raw[t], "w%d" % t)
-
-        dk_grouped = keep.tile([P, SLOTS, LANES], BF16, name="dk_grouped", tag="late", align_bytes=64)
-        interleave(dk_grouped, dk_rows, DK_VECTOR_COLS)
         dk_codes = keep.tile([P, SLOTS], U32, name="dk_codes", align_bytes=64)
         dk_scales = keep.tile([P, SLOTS], U8, name="dk_scales", align_bytes=64)
-        nc.vector.quantize_mx(
-            out=dk_codes[:].bitcast(E5M2), scales=dk_scales[:], in_=dk_grouped[:].rearrange("p c t -> p (c t)"))
+        w_codes = keep.tile([P, K], U32, name="w_codes", align_bytes=64)
+        w_scales = keep.tile([P, K], U8, name="w_scales", align_bytes=64)
 
-        late_window = keep.tile([P, TOKENS], F32, name="window2", tag="late", align_bytes=64)
-        nc.vector.memset(late_window[:].bitcast(I32), 0)
-        windows.append(late_window)
+        def g_operand(s):
+            cols = slice(s * P, (s + 1) * P)
+            g_grouped = stage("g_grouped%d" % s, "q_paired%d" % (2 + s % 2))
+            src = g_raw[s // 2][:, :, (s % 2) * P : (s % 2 + 1) * P]
+            copy = nc.vector.tensor_copy if s == 0 else nc.scalar.copy
+            copy(g_grouped[:].rearrange("p (c i t) -> p c t i", i=4, t=LANES), src.rearrange("p t (c i) -> p c t i", i=4))
+            nc.vector.quantize_mx(out=g_codes[:, cols].bitcast(E5M2), scales=g_scales[:, cols], in_=g_grouped[:])
+
+        def dk_operand(s):
+            cols = slice(s * P, (s + 1) * P)
+            acc = psum.tile([P, K], F32, name="acc%d" % s)
+            nc.tensor.matmul_mx(
+                out=acc[:], lhsT=g_codes[:, cols].bitcast(E5M2), lhsT_scale=g_scales[:, cols],
+                rhs=q_codes[:].bitcast(E4M3), rhs_scale=q_scales[:], start=True, stop=True)
+            dk_paired = stage("dk_paired%d" % s, "dk_paired%d" % s)
+            nc.vector.scalar_tensor_tensor(
+                out=dk_paired[:], in0=acc[:], scalar=ts_cols[:, s : s + 1], in1=cf_all[:], op0=MULT, op1=MULT)
+            dk_grouped = stage("dk_grouped%d" % s, "dk_grouped%d" % s)
+            turn_words(dk_paired[:], dk_grouped[:])
+            nc.vector.quantize_mx(out=dk_codes[:, cols].bitcast(E5M2), scales=dk_scales[:, cols], in_=dk_grouped[:])
+
+        w_order = "m (p e u) -> m u p e"
+        w_tags = ["q_paired3", "dk_paired1", "dk_grouped3", "dk_grouped2"]
+
+        def w_round(t, round_copy):
+            paired = stage("w_paired%d" % t, w_tags[t])
+            round_pairs(round_copy, w_raw[t], w_order, paired)
+            return paired
+
+        def w_quantise(first, grouped):
+            cols = slice(first * P, first * P + grouped.shape[1] // LANES)
+            nc.vector.quantize_mx(out=w_codes[:, cols].bitcast(E4M3), scales=w_scales[:, cols], in_=grouped[:])
+
+        for h in range(2):
+            for s in (2 * h, 2 * h + 1):
+                g_operand(s)
+            for s in (2 * h, 2 * h + 1):
+                dk_operand(s)
+        for t in (0, 1):
+            paired = w_round(t, nc.scalar.copy)
+            grouped = stage("w_grouped%d" % t, "w_grouped%d" % t)
+            turn_words(paired[:], grouped[:])
+            w_quantise(t, grouped)
 
         dc = []
 
         def product(t):
+            cols = slice(t * P, (t + 1) * P)
             acc = psum.tile([P, SLOTS], F32, name="acc%d" % t)
             nc.tensor.matmul_mx(
-                out=acc[:], lhsT=w_ops[t][0][:].bitcast(E4M3), lhsT_scale=w_ops[t][1][:],
+                out=acc[:], lhsT=w_codes[:, cols].bitcast(E4M3), lhsT_scale=w_scales[:, cols],
                 rhs=dk_codes[:].bitcast(E5M2), rhs_scale=dk_scales[:], start=True, stop=True)
-            dc_t = keep.tile([P, SLOTS], F32, name="dc%d" % t)
+            tag = "late2" if t == 0 else "dc%d" % t
+            dc_t = keep.tile([P, SLOTS], F32, name="dc%d" % t, tag=tag)
             nc.scalar.copy(dc_t[:], acc[:])
             dc.append(dc_t)
 
-        for t in (0, 1):
-            product(t)
+        product(0)
+        late_grouped = keep.tile([P, 2 * K], BF16, name="late_grouped", align_bytes=64)
         for t in (2, 3):
-            w_ops[t] = stationary(w_raw[t], "w%d" % t)
-        for t in (2, 3):
+            paired = w_round(t, nc.vector.tensor_copy)
+            turn_words(paired[:], late_grouped[:, (t - 2) * K : (t - 1) * K])
+        w_quantise(2, late_grouped)
+        for t in (1, 2, 3):
             product(t)
+
+        window1 = keep.tile([P, TOKENS], F32, name="window1", tag="dk_grouped3", align_bytes=64)
+        nc.gpsimd.memset(window1[:].bitcast(I32), 0)
+        windows.append(window1)
 
         out_rows = out_0.rearrange("(p t) c -> p t c", t=LANES)
         pairs = [keep.tile([P, 2, CHUNK, 2], BF16, name="pairs%d" % c, align_bytes=64) for c in range(CHUNKS)]
@@ -179,6 +193,10 @@ def tile_attend_gmla_c_pl_kernel(tc, qT, G, wk, ts, cf, offs, out_0, out_1, out_
         for t in range(LANES):
             window = windows[t % 3]
             nc.vector.tensor_copy(window[:].indirect(offsets[:]), dc[t][:])
+            if t == 0:
+                window2 = keep.tile([P, TOKENS], F32, name="window2", tag="late2")
+                nc.gpsimd.memset(window2[:].bitcast(I32), 0)
+                windows.append(window2)
             nc.sync.dma_start(out_rows[:, t, :], window[:])
             if t < LANES - 1:
                 for c in range(CHUNKS):

@@ -12,6 +12,7 @@ U8 = mybir.dt.uint8
 E4M3 = mybir.dt.float8_e4m3fn_x4
 E5M2 = mybir.dt.float8_e5m2_x4
 MULT = mybir.AluOpType.mult
+ADD = mybir.AluOpType.add
 
 P = 128
 LANES = 4
@@ -21,7 +22,7 @@ TILES = SLOTS // P
 TOKENS = 2048
 CHUNK = 512
 CHUNKS = TOKENS // CHUNK
-G_HALF = SLOTS // 2
+HALF = SLOTS // 2
 TS_ROW = P - 1
 
 FLOPS = 2 * 2 * 512 * 512 * 512
@@ -34,155 +35,198 @@ def tile_attend_gmla_c_pl_kernel(tc, qT, G, wk, ts, cf, offs, out_0, out_1, out_
         psum = ctx.enter_context(tc.psum_pool(name="psum", bufs=1))
         turn = ctx.enter_context(tc.psum_pool(name="turn", bufs=4))
 
-        q_rows = qT.rearrange("(h m u) r -> u h m r", h=2, u=2)
+        q_rows = qT.rearrange("(h m u) r -> h m u r", h=2, u=2)
         w_rows = wk.rearrange("(m t) f -> m t f", t=LANES)
         g_rows = G.rearrange("(p j) i -> p j i", j=LANES)
-        q_raw = [keep.tile([P, K], F32, name="q_raw%d" % t) for t in range(LANES)]
-        w_raw = [keep.tile([P, K], F32, name="w_raw%d" % t) for t in range(LANES)]
-        g_raw = [keep.tile([P, LANES, G_HALF], F32, name="g_raw%d" % h) for h in range(2)]
+        q_raw = [keep.tile([P, 2, K], F32, name="q_raw%d" % h) for h in range(2)]
+        w_raw = [keep.tile([P, K], F32, name="w_raw%d" % t) for t in range(2)]
+        w_late_raw = keep.tile([P, 2, K], F32, name="w_late_raw")
+        g_raw = [keep.tile([P, LANES, HALF], F32, name="g_raw%d" % h) for h in range(2)]
         offsets = keep.tile([P, SLOTS // 16], U16, name="offsets")
         ts_window = keep.tile([P, TOKENS], F32, name="ts_window")
         cf_cols = keep.tile([P, LANES], F32, name="cf_cols")
 
-        nc.scalar.dma_start(ts_window[TS_ROW:P, :], ts[0:1, :])
-        nc.scalar.dma_start(cf_cols[:], cf.rearrange("(p t) o -> p (t o)", t=LANES))
-        nc.sync.dma_start(q_raw[0][:], q_rows[0, 0])
+        nc.scalar.dma_start(q_raw[0][:], q_rows[0])
+        nc.sync.dma_start(cf_cols[:], cf.rearrange("(p t) o -> p (t o)", t=LANES))
+        nc.sync.dma_start(ts_window[TS_ROW:P, :], ts[0:1, :])
         nc.sync.dma_start(offsets[:], offs)
-        for t in range(1, LANES):
-            nc.sync.dma_start(q_raw[t][:], q_rows[t // 2, t % 2])
-        for h in range(2):
-            nc.sync.dma_start(g_raw[h][:], g_rows[:, :, h * G_HALF : (h + 1) * G_HALF])
-        for t in range(LANES):
-            nc.sync.dma_start(w_raw[t][:], w_rows[:, t, :])
+        nc.sync.dma_start(q_raw[1][:], q_rows[1])
+        nc.sync.dma_start(g_raw[0][:], g_rows[:, :, :HALF])
+        nc.sync.dma_start(w_raw[0][:], w_rows[:, 0, :])
+        nc.sync.dma_start(g_raw[1][:], g_rows[:, :, HALF:])
+        nc.sync.dma_start(w_raw[1][:], w_rows[:, 1, :])
+        nc.sync.dma_start(w_late_raw[:], w_rows[:, 2:, :])
 
         ident = keep.tile([P, P], F32, name="ident")
         make_identity(nc, ident[:])
 
         nc.vector.memset(ts_window[0:TS_ROW, :].bitcast(I32), 0)
-        windows = [keep.tile([P, TOKENS], F32, name="window0")]
-        nc.gpsimd.memset(windows[0][:].bitcast(I32), 0)
 
-        def turn_words(paired, grouped):
-            words = paired.bitcast(F32)
-            turned = turn.tile([P, 2, P], F32, name="turned")
-            for u in range(2):
-                nc.tensor.transpose(turned[:, u, :], words[:, u * P : (u + 1) * P], ident[:])
-            nc.scalar.copy(
-                grouped.bitcast(F32).rearrange("p (m u) -> p m u", u=2),
-                turned[:].rearrange("p u m -> p m u"),
-            )
+        def zeroed_window(name, tag):
+            window = keep.tile([P, TOKENS], F32, name=name, tag=tag, align_bytes=64)
+            nc.gpsimd.memset(window[:].bitcast(I32), 0)
+            return window
 
-        def stage(name, tag):
-            return keep.tile([P, K], BF16, name=name, tag=tag, align_bytes=64)
+        windows = [zeroed_window("window0", "window0")]
+
+        def stage(name, tag, width=K):
+            return keep.tile([P, width], BF16, name=name, tag=tag, align_bytes=64)
 
         def round_pairs(round_copy, raw, order, paired):
-            round_copy(paired[:].rearrange("m (u p e) -> m u p e", u=2, e=2), raw[:].rearrange(order, u=2, e=2))
+            round_copy(paired[:].rearrange("m (u p e) -> m u p e", u=2, e=2), raw.rearrange(order, u=2, e=2))
+
+        def turn_words(paired, grouped):
+            words = paired[:].bitcast(F32)
+            blocks = words.shape[1] // P
+            turned = turn.tile([P, blocks, P], F32, name="turned")
+            for block in range(blocks):
+                nc.tensor.transpose(turned[:, block, :], words[:, block * P : (block + 1) * P], ident[:])
+            nc.scalar.copy(
+                grouped.bitcast(F32).rearrange("p (t m u) -> p t m u", m=P, u=2),
+                turned[:].rearrange("p (t u) m -> p t m u", u=2),
+            )
 
         ts_row = keep.tile([P, SLOTS], F32, name="ts_row")
         nc.vector.tensor_copy(ts_row[:], ts_window[:].indirect(offsets[:]))
 
+        cf_wide = keep.tile([P, LANES, P], F32, name="cf_wide")
+        nc.scalar.copy(cf_wide[:], cf_cols[:].unsqueeze(2).to_broadcast([P, LANES, P]))
+        cf_turned = turn.tile([P, LANES, P], F32, name="turned")
+        for t in range(LANES):
+            nc.tensor.transpose(cf_turned[:, t, :], cf_wide[:, t, :], ident[:])
+
         q_codes = keep.tile([P, K], U32, name="q_codes", align_bytes=64)
         q_scales = keep.tile([P, K], U8, name="q_scales", align_bytes=64)
-        for t in range(LANES):
+
+        def q_operand(h, u, round_copy):
+            t = 2 * u + h
             cols = slice(t * P, (t + 1) * P)
-            round_copy = nc.scalar.copy if t % 2 == 0 else nc.vector.tensor_copy
             paired = stage("q_paired%d" % t, "q_paired%d" % t)
-            round_pairs(round_copy, q_raw[t], "m (p u e) -> m u p e", paired)
+            round_pairs(round_copy, q_raw[h][:, u, :], "m (p u e) -> m u p e", paired)
             grouped = stage("q_grouped%d" % t, "q_grouped%d" % t)
-            turn_words(paired[:], grouped[:])
+            turn_words(paired, grouped[:])
             nc.vector.quantize_mx(out=q_codes[:, cols].bitcast(E4M3), scales=q_scales[:, cols], in_=grouped[:])
 
+        q_operand(0, 0, nc.scalar.copy)
+        q_operand(0, 1, nc.vector.tensor_copy)
+        q_operand(1, 0, nc.vector.tensor_copy)
+        q_operand(1, 1, nc.vector.tensor_copy)
+
+        cf_all = keep.tile([P, K], F32, name="cf_all")
+        nc.scalar.copy(
+            cf_all[:].rearrange("i (u p e) -> i u p e", u=2, e=2),
+            cf_turned[:].rearrange("i (e u) p -> i u p e", u=2),
+        )
         ts_turned = turn.tile([P, TILES, P], F32, name="turned")
         for s in range(TILES):
             nc.tensor.transpose(ts_turned[:, s, :], ts_row[:, s * P : (s + 1) * P], ident[:])
         ts_cols = keep.tile([P, TILES], F32, name="ts_cols")
-        nc.vector.tensor_copy(ts_cols[:], ts_turned[:, :, TS_ROW])
+        nc.scalar.copy(ts_cols[:], ts_turned[:, :, TS_ROW])
 
-        cf_turned = turn.tile([P, LANES, P], F32, name="turned")
-        for t in range(LANES):
-            nc.tensor.transpose(cf_turned[:, t, :], cf_cols[:, t : t + 1].to_broadcast([P, P]), ident[:])
-        cf_all = keep.tile([P, K], F32, name="cf_all")
-        nc.vector.tensor_copy(
-            cf_all[:].rearrange("i (u p e) -> i u p e", u=2, e=2),
-            cf_turned[:].rearrange("i (e u) p -> i u p e", u=2),
-        )
-
-        g_codes = keep.tile([P, SLOTS], U32, name="g_codes", align_bytes=64)
-        g_scales = keep.tile([P, SLOTS], U8, name="g_scales", align_bytes=64)
-        dk_codes = keep.tile([P, SLOTS], U32, name="dk_codes", align_bytes=64)
-        dk_scales = keep.tile([P, SLOTS], U8, name="dk_scales", align_bytes=64)
+        grad_codes = keep.tile([P, 2 * SLOTS], U32, name="grad_codes", align_bytes=64)
+        grad_scales = keep.tile([P, 2 * SLOTS], U8, name="grad_scales", align_bytes=64)
         w_codes = keep.tile([P, K], U32, name="w_codes", align_bytes=64)
         w_scales = keep.tile([P, K], U8, name="w_scales", align_bytes=64)
 
-        def g_operand(s):
-            cols = slice(s * P, (s + 1) * P)
-            g_grouped = stage("g_grouped%d" % s, "q_paired%d" % (2 + s % 2))
-            src = g_raw[s // 2][:, :, (s % 2) * P : (s % 2 + 1) * P]
-            copy = nc.vector.tensor_copy if s == 0 else nc.scalar.copy
-            copy(g_grouped[:].rearrange("p (c i t) -> p c t i", i=4, t=LANES), src.rearrange("p t (c i) -> p c t i", i=4))
-            nc.vector.quantize_mx(out=g_codes[:, cols].bitcast(E5M2), scales=g_scales[:, cols], in_=g_grouped[:])
+        def g_cols(s):
+            return slice((s + 2) % TILES * P, ((s + 2) % TILES + 1) * P)
 
-        def dk_operand(s):
-            cols = slice(s * P, (s + 1) * P)
+        def quantise_grad(cols, grouped):
+            nc.vector.quantize_mx(out=grad_codes[:, cols].bitcast(E5M2), scales=grad_scales[:, cols], in_=grouped[:])
+
+        def g_interleave(s, copy, tag):
+            grouped = stage("g_grouped%d" % s, tag)
+            src = g_raw[s // 2][:, :, (s % 2) * P : (s % 2 + 1) * P]
+            copy(grouped[:].rearrange("p (c i t) -> p c t i", i=4, t=LANES), src.rearrange("p t (c i) -> p c t i", i=4))
+            return grouped
+
+        def first_product(s):
             acc = psum.tile([P, K], F32, name="acc%d" % s)
             nc.tensor.matmul_mx(
-                out=acc[:], lhsT=g_codes[:, cols].bitcast(E5M2), lhsT_scale=g_scales[:, cols],
+                out=acc[:], lhsT=grad_codes[:, g_cols(s)].bitcast(E5M2), lhsT_scale=grad_scales[:, g_cols(s)],
                 rhs=q_codes[:].bitcast(E4M3), rhs_scale=q_scales[:], start=True, stop=True)
-            dk_paired = stage("dk_paired%d" % s, "dk_paired%d" % s)
+            return acc
+
+        def dk_pairs(s, acc):
+            paired = stage("dk_paired%d" % s, "dk_paired%d" % s)
             nc.vector.scalar_tensor_tensor(
-                out=dk_paired[:], in0=acc[:], scalar=ts_cols[:, s : s + 1], in1=cf_all[:], op0=MULT, op1=MULT)
-            dk_grouped = stage("dk_grouped%d" % s, "dk_grouped%d" % s)
-            turn_words(dk_paired[:], dk_grouped[:])
-            nc.vector.quantize_mx(out=dk_codes[:, cols].bitcast(E5M2), scales=dk_scales[:, cols], in_=dk_grouped[:])
+                out=paired[:], in0=acc[:], scalar=ts_cols[:, s : s + 1], in1=cf_all[:], op0=MULT, op1=MULT)
+            return paired
 
-        w_order = "m (p e u) -> m u p e"
-        w_tags = ["q_paired3", "dk_paired1", "dk_grouped3", "dk_grouped2"]
-
-        def w_round(t, round_copy):
-            paired = stage("w_paired%d" % t, w_tags[t])
-            round_pairs(round_copy, w_raw[t], w_order, paired)
+        def w_pairs(t, raw, round_copy, tag):
+            paired = stage("w_paired%d" % t, tag)
+            round_pairs(round_copy, raw, "m (p e u) -> m u p e", paired)
             return paired
 
         def w_quantise(first, grouped):
             cols = slice(first * P, first * P + grouped.shape[1] // LANES)
             nc.vector.quantize_mx(out=w_codes[:, cols].bitcast(E4M3), scales=w_scales[:, cols], in_=grouped[:])
 
-        for h in range(2):
-            for s in (2 * h, 2 * h + 1):
-                g_operand(s)
-            for s in (2 * h, 2 * h + 1):
-                dk_operand(s)
-        for t in (0, 1):
-            paired = w_round(t, nc.scalar.copy)
-            grouped = stage("w_grouped%d" % t, "w_grouped%d" % t)
-            turn_words(paired[:], grouped[:])
-            w_quantise(t, grouped)
-
-        dc = []
-
-        def product(t):
+        def product(t, first, bank):
             cols = slice(t * P, (t + 1) * P)
-            acc = psum.tile([P, SLOTS], F32, name="acc%d" % t)
+            moving = slice(first, first + SLOTS)
+            acc = psum.tile([P, SLOTS], F32, name="acc%d" % bank)
             nc.tensor.matmul_mx(
                 out=acc[:], lhsT=w_codes[:, cols].bitcast(E4M3), lhsT_scale=w_scales[:, cols],
-                rhs=dk_codes[:].bitcast(E5M2), rhs_scale=dk_scales[:], start=True, stop=True)
-            tag = "late2" if t == 0 else "dc%d" % t
-            dc_t = keep.tile([P, SLOTS], F32, name="dc%d" % t, tag=tag)
-            nc.scalar.copy(dc_t[:], acc[:])
-            dc.append(dc_t)
+                rhs=grad_codes[:, moving].bitcast(E5M2), rhs_scale=grad_scales[:, moving], start=True, stop=True)
+            return acc
 
-        product(0)
-        late_grouped = keep.tile([P, 2 * K], BF16, name="late_grouped", align_bytes=64)
-        for t in (2, 3):
-            paired = w_round(t, nc.vector.tensor_copy)
-            turn_words(paired[:], late_grouped[:, (t - 2) * K : (t - 1) * K])
-        w_quantise(2, late_grouped)
-        for t in (1, 2, 3):
-            product(t)
+        def copy_out(name, tag, part):
+            dc = keep.tile([P, part.shape[1]], F32, name=name, tag=tag, align_bytes=64)
+            nc.scalar.copy(dc[:], part)
+            return dc
 
-        window1 = keep.tile([P, TOKENS], F32, name="window1", tag="dk_grouped3", align_bytes=64)
-        nc.gpsimd.memset(window1[:].bitcast(I32), 0)
-        windows.append(window1)
+        def scatter(window, first, dc):
+            entries = offsets[:, first // 16 : (first + dc.shape[1]) // 16]
+            nc.vector.tensor_copy(window[:].indirect(entries), dc[:])
+
+        dk_early = stage("dk_early", "dk_early", 2 * K)
+        dk_late = stage("dk_late", "dk_late", 2 * K)
+        w_grouped = [stage("w_grouped%d" % t, "w_grouped%d" % t) for t in range(2)]
+        w_late = stage("w_late", "w_late", 2 * K)
+
+        quantise_grad(g_cols(0), g_interleave(0, nc.vector.tensor_copy, "q_paired1"))
+        quantise_grad(g_cols(1), g_interleave(1, nc.scalar.copy, "q_paired3"))
+        b = [first_product(0), first_product(1)]
+        w0 = w_pairs(0, w_raw[0][:], nc.scalar.copy, "q_grouped1")
+        g2 = g_interleave(2, nc.scalar.copy, "q_grouped3")
+        dk = [dk_pairs(0, b[0]), dk_pairs(1, b[1])]
+        turn_words(w0, w_grouped[0][:])
+        turn_words(dk[0], dk_early[:, :K])
+        turn_words(dk[1], dk_early[:, K:])
+        g3 = g_interleave(3, nc.vector.tensor_copy, "dk_paired0")
+        quantise_grad(g_cols(2), g2)
+        w_quantise(0, w_grouped[0])
+        quantise_grad(g_cols(3), g3)
+        b.extend([first_product(2), first_product(3)])
+        quantise_grad(slice(SLOTS, SLOTS + HALF), dk_early)
+        windows.append(zeroed_window("window1", "dk_early"))
+        w1 = w_pairs(1, w_raw[1][:], nc.vector.tensor_copy, "dk_paired0")
+        w23 = stage("w_paired23", "dk_paired1", 2 * K)
+        nc.scalar.copy(
+            w23[:].rearrange("m (t u p e) -> m t u p e", t=2, u=2, e=2),
+            w_late_raw[:].rearrange("m t (p e u) -> m t u p e", u=2, e=2))
+        early_acc0 = product(0, HALF, 0)
+        dk.extend([dk_pairs(2, b[2]), dk_pairs(3, b[3])])
+        turn_words(w1, w_grouped[1][:])
+        w_quantise(1, w_grouped[1])
+        early0 = copy_out("early0", "dk_paired0", early_acc0[:, HALF:])
+        turn_words(dk[2], dk_late[:, :K])
+        early_acc1 = product(1, HALF, 1)
+        turn_words(dk[3], dk_late[:, K:])
+        turn_words(w23, w_late[:])
+        scatter(windows[0], 0, early0)
+        quantise_grad(slice(SLOTS + HALF, 2 * SLOTS), dk_late)
+        w_quantise(2, w_late)
+        early1 = copy_out("early1", "dk_paired1", early_acc1[:, HALF:])
+        scatter(windows[1], 0, early1)
+        windows.append(zeroed_window("window2", "dk_late"))
+        rest = [
+            copy_out("late0", "late0", product(0, SLOTS, 2)[:, HALF:]),
+            copy_out("late1", "late1", product(1, SLOTS, 3)[:, HALF:]),
+            copy_out("dc2", "dc2", product(2, SLOTS, 0)[:]),
+            copy_out("dc3", "dc3", product(3, SLOTS, 1)[:]),
+        ]
 
         out_rows = out_0.rearrange("(p t) c -> p t c", t=LANES)
         pairs = [keep.tile([P, 2, CHUNK, 2], BF16, name="pairs%d" % c, align_bytes=64) for c in range(CHUNKS)]
@@ -190,20 +234,24 @@ def tile_attend_gmla_c_pl_kernel(tc, qT, G, wk, ts, cf, offs, out_0, out_1, out_
         def round_lane(engine_copy, t, c):
             engine_copy(pairs[c][:, t // 2, :, t % 2], windows[t % 3][:, c * CHUNK : (c + 1) * CHUNK])
 
+        def round_both(engine_copy, c):
+            engine_copy(pairs[c][:, 1], windows[2][:, c * CHUNK : (c + 1) * CHUNK].unsqueeze(2).to_broadcast([P, CHUNK, 2]))
+
+        def gpsimd_round(out, in_):
+            nc.gpsimd.tensor_scalar(out=out, in0=in_, scalar1=1.0, scalar2=0.0, op0=MULT, op1=ADD)
+
         for t in range(LANES):
             window = windows[t % 3]
-            nc.vector.tensor_copy(window[:].indirect(offsets[:]), dc[t][:])
-            if t == 0:
-                window2 = keep.tile([P, TOKENS], F32, name="window2", tag="late2")
-                nc.gpsimd.memset(window2[:].bitcast(I32), 0)
-                windows.append(window2)
+            scatter(window, SLOTS - rest[t].shape[1], rest[t])
             nc.sync.dma_start(out_rows[:, t, :], window[:])
-            if t < LANES - 1:
+            if t < 2:
                 for c in range(CHUNKS):
-                    if (t, c) == (LANES - 2, 0):
-                        nc.scalar.copy(pairs[0][:, 1], window[:, :CHUNK].unsqueeze(2).to_broadcast([P, CHUNK, 2]))
-                    else:
-                        round_lane(nc.scalar.copy, t, c)
+                    round_lane(nc.scalar.copy if c < 2 else gpsimd_round, t, c)
+            if t == 2:
+                round_both(nc.scalar.copy, 0)
+                round_both(gpsimd_round, CHUNKS - 1)
+                for c in range(1, CHUNKS - 1):
+                    round_lane(nc.scalar.copy, t, c)
 
         last = LANES - 1
         words_out = out_1[0].rearrange("p c l -> p (c l)").bitcast(I32)

@@ -20,8 +20,12 @@ K = 512
 SLOTS = 512
 TILES = SLOTS // P
 TOKENS = 2048
-CHUNK = 512
-CHUNKS = TOKENS // CHUNK
+CHUNKS = [512, 512, 512, 512]
+LAST_PIECE = 256
+SLOT_A = 18432
+SLOT_B = SLOT_A + 1024
+SCALAR_EARLY = 832
+VECTOR_LAST = 896
 HALF = SLOTS // 2
 TS_ROW = P - 1
 
@@ -34,51 +38,61 @@ def tile_attend_gmla_c_pl_kernel(tc, qT, G, wk, ts, cf, offs, out_0, out_1, out_
         keep = ctx.enter_context(tc.tile_pool(name="keep", bufs=1))
         psum = ctx.enter_context(tc.psum_pool(name="psum", bufs=1))
         turn = ctx.enter_context(tc.psum_pool(name="turn", bufs=4))
+        placed = ctx.enter_context(tc.tile_pool(name="placed", bufs=1))
 
         q_rows = qT.rearrange("(h m u) r -> h m u r", h=2, u=2)
         w_rows = wk.rearrange("(m t) f -> m t f", t=LANES)
         g_rows = G.rearrange("(p j) i -> p j i", j=LANES)
-        q_raw = [keep.tile([P, 2, K], F32, name="q_raw%d" % h) for h in range(2)]
-        w_raw = [keep.tile([P, K], F32, name="w_raw%d" % t) for t in range(2)]
-        w_late_raw = keep.tile([P, 2, K], F32, name="w_late_raw")
+        q_first = keep.tile([P, 2, K], F32, name="q_first")
+        q_second = [keep.tile([P, K], F32, name="q_second%d" % u) for u in range(2)]
+        q_raw = [[q_first[:, u, :] for u in range(2)], [q_second[u][:] for u in range(2)]]
+        w_raw = [keep.tile([P, 2, K], F32, name="w_raw%d" % h) for h in range(2)]
         g_raw = [keep.tile([P, LANES, HALF], F32, name="g_raw%d" % h) for h in range(2)]
         offsets = keep.tile([P, SLOTS // 16], U16, name="offsets")
         ts_window = keep.tile([P, TOKENS], F32, name="ts_window")
         cf_cols = keep.tile([P, LANES], F32, name="cf_cols")
 
-        nc.scalar.dma_start(q_raw[0][:], q_rows[0])
+        nc.scalar.dma_start(q_first[:], q_rows[0])
         nc.sync.dma_start(cf_cols[:], cf.rearrange("(p t) o -> p (t o)", t=LANES))
         nc.sync.dma_start(ts_window[TS_ROW:P, :], ts[0:1, :])
         nc.sync.dma_start(offsets[:], offs)
-        nc.sync.dma_start(q_raw[1][:], q_rows[1])
+        for u in range(2):
+            nc.sync.dma_start(q_raw[1][u], q_rows[1, :, u, :])
         nc.sync.dma_start(g_raw[0][:], g_rows[:, :, :HALF])
-        nc.sync.dma_start(w_raw[0][:], w_rows[:, 0, :])
         nc.sync.dma_start(g_raw[1][:], g_rows[:, :, HALF:])
-        nc.sync.dma_start(w_raw[1][:], w_rows[:, 1, :])
-        nc.sync.dma_start(w_late_raw[:], w_rows[:, 2:, :])
+        nc.sync.dma_start(w_raw[0][:], w_rows[:, :2, :])
+        nc.sync.dma_start(w_raw[1][:], w_rows[:, 2:, :])
 
         ident = keep.tile([P, P], F32, name="ident")
         make_identity(nc, ident[:])
 
         nc.vector.memset(ts_window[0:TS_ROW, :].bitcast(I32), 0)
 
-        def zeroed_window(name, tag):
-            window = keep.tile([P, TOKENS], F32, name=name, tag=tag, align_bytes=64)
+        def zeroed_window(name, tag, offset=None):
+            if offset is None:
+                window = keep.tile([P, TOKENS], F32, name=name, tag=tag, align_bytes=64)
+            else:
+                window = placed.tile([P, TOKENS], F32, name=name, offset=offset, align_bytes=64)
             nc.gpsimd.memset(window[:].bitcast(I32), 0)
             return window
 
         windows = [zeroed_window("window0", "window0")]
 
-        def stage(name, tag, width=K):
-            return keep.tile([P, width], BF16, name=name, tag=tag, align_bytes=64)
+        def stage(name, tag, width=K, offset=None):
+            if offset is None:
+                return keep.tile([P, width], BF16, name=name, tag=tag, align_bytes=64)
+            return placed.tile([P, width], BF16, name=name, offset=offset, align_bytes=64)
 
         def round_pairs(round_copy, raw, order, paired):
             round_copy(paired[:].rearrange("m (u p e) -> m u p e", u=2, e=2), raw.rearrange(order, u=2, e=2))
 
-        def turn_words(paired, grouped):
-            words = paired[:].bitcast(F32)
+        def turn_words(paired, grouped, bank=None):
+            words = paired.bitcast(F32)
             blocks = words.shape[1] // P
-            turned = turn.tile([P, blocks, P], F32, name="turned")
+            if bank is None:
+                turned = turn.tile([P, blocks, P], F32, name="turned")
+            else:
+                turned = psum.tile([P, blocks, P], F32, name="acc%d" % bank)
             for block in range(blocks):
                 nc.tensor.transpose(turned[:, block, :], words[:, block * P : (block + 1) * P], ident[:])
             nc.scalar.copy(
@@ -95,33 +109,35 @@ def tile_attend_gmla_c_pl_kernel(tc, qT, G, wk, ts, cf, offs, out_0, out_1, out_
         for t in range(LANES):
             nc.tensor.transpose(cf_turned[:, t, :], cf_wide[:, t, :], ident[:])
 
+        cf_all = keep.tile([P, K], F32, name="cf_all")
+        nc.scalar.copy(
+            cf_all[:].rearrange("i (u p e) -> i u p e", u=2, e=2),
+            cf_turned[:].rearrange("i (e u) p -> i u p e", u=2),
+        )
+
         q_codes = keep.tile([P, K], U32, name="q_codes", align_bytes=64)
         q_scales = keep.tile([P, K], U8, name="q_scales", align_bytes=64)
 
         def q_operand(h, u, round_copy):
             t = 2 * u + h
             cols = slice(t * P, (t + 1) * P)
-            paired = stage("q_paired%d" % t, "q_paired%d" % t)
-            round_pairs(round_copy, q_raw[h][:, u, :], "m (p u e) -> m u p e", paired)
-            grouped = stage("q_grouped%d" % t, "q_grouped%d" % t)
-            turn_words(paired, grouped[:])
+            paired = stage("q_paired%d" % t, "q_paired%d" % t, offset=SLOT_B if t == 3 else None)
+            round_pairs(round_copy, q_raw[h][u], "m (p u e) -> m u p e", paired)
+            grouped = stage("q_grouped%d" % t, "q_grouped%d" % t, offset=SLOT_A if t == 1 else None)
+            turn_words(paired[:], grouped[:])
             nc.vector.quantize_mx(out=q_codes[:, cols].bitcast(E4M3), scales=q_scales[:, cols], in_=grouped[:])
 
         q_operand(0, 0, nc.scalar.copy)
         q_operand(0, 1, nc.vector.tensor_copy)
-        q_operand(1, 0, nc.vector.tensor_copy)
-        q_operand(1, 1, nc.vector.tensor_copy)
 
-        cf_all = keep.tile([P, K], F32, name="cf_all")
-        nc.scalar.copy(
-            cf_all[:].rearrange("i (u p e) -> i u p e", u=2, e=2),
-            cf_turned[:].rearrange("i (e u) p -> i u p e", u=2),
-        )
         ts_turned = turn.tile([P, TILES, P], F32, name="turned")
         for s in range(TILES):
             nc.tensor.transpose(ts_turned[:, s, :], ts_row[:, s * P : (s + 1) * P], ident[:])
         ts_cols = keep.tile([P, TILES], F32, name="ts_cols")
         nc.scalar.copy(ts_cols[:], ts_turned[:, :, TS_ROW])
+
+        q_operand(1, 0, nc.vector.tensor_copy)
+        q_operand(1, 1, nc.vector.tensor_copy)
 
         grad_codes = keep.tile([P, 2 * SLOTS], U32, name="grad_codes", align_bytes=64)
         grad_scales = keep.tile([P, 2 * SLOTS], U8, name="grad_scales", align_bytes=64)
@@ -134,8 +150,11 @@ def tile_attend_gmla_c_pl_kernel(tc, qT, G, wk, ts, cf, offs, out_0, out_1, out_
         def quantise_grad(cols, grouped):
             nc.vector.quantize_mx(out=grad_codes[:, cols].bitcast(E5M2), scales=grad_scales[:, cols], in_=grouped[:])
 
-        def g_interleave(s, copy, tag):
-            grouped = stage("g_grouped%d" % s, tag)
+        def gpsimd_round(out, in_):
+            nc.gpsimd.tensor_scalar(out=out, in0=in_, scalar1=1.0, scalar2=0.0, op0=MULT, op1=ADD)
+
+        def g_interleave(s, copy, tag, offset=None):
+            grouped = stage("g_grouped%d" % s, tag, offset=offset)
             src = g_raw[s // 2][:, :, (s % 2) * P : (s % 2 + 1) * P]
             copy(grouped[:].rearrange("p (c i t) -> p c t i", i=4, t=LANES), src.rearrange("p t (c i) -> p c t i", i=4))
             return grouped
@@ -148,19 +167,22 @@ def tile_attend_gmla_c_pl_kernel(tc, qT, G, wk, ts, cf, offs, out_0, out_1, out_
             return acc
 
         def dk_pairs(s, acc):
-            paired = stage("dk_paired%d" % s, "dk_paired%d" % s)
+            paired = stage("dk_paired%d" % s, "dk_paired%d" % s, offset=SLOT_B + 512 if s == 0 else None)
             nc.vector.scalar_tensor_tensor(
                 out=paired[:], in0=acc[:], scalar=ts_cols[:, s : s + 1], in1=cf_all[:], op0=MULT, op1=MULT)
             return paired
 
-        def w_pairs(t, raw, round_copy, tag):
-            paired = stage("w_paired%d" % t, tag)
-            round_pairs(round_copy, raw, "m (p e u) -> m u p e", paired)
+        def w_pairs(first, count, tag, offset=None):
+            paired = stage("w_paired%d" % first, tag, count * K, offset)
+            raw = w_raw[first // 2][:, first % 2 : first % 2 + count, :]
+            nc.scalar.copy(
+                paired[:].rearrange("m (t u p e) -> m t u p e", t=count, u=2, e=2),
+                raw.rearrange("m t (p e u) -> m t u p e", u=2, e=2))
             return paired
 
         def w_quantise(first, grouped):
             cols = slice(first * P, first * P + grouped.shape[1] // LANES)
-            nc.vector.quantize_mx(out=w_codes[:, cols].bitcast(E4M3), scales=w_scales[:, cols], in_=grouped[:])
+            nc.vector.quantize_mx(out=w_codes[:, cols].bitcast(E4M3), scales=w_scales[:, cols], in_=grouped)
 
         def product(t, first, bank):
             cols = slice(t * P, (t + 1) * P)
@@ -171,9 +193,9 @@ def tile_attend_gmla_c_pl_kernel(tc, qT, G, wk, ts, cf, offs, out_0, out_1, out_
                 rhs=grad_codes[:, moving].bitcast(E5M2), rhs_scale=grad_scales[:, moving], start=True, stop=True)
             return acc
 
-        def copy_out(name, tag, part):
-            dc = keep.tile([P, part.shape[1]], F32, name=name, tag=tag, align_bytes=64)
-            nc.scalar.copy(dc[:], part)
+        def copy_out(name, copy, part):
+            dc = keep.tile([P, part.shape[1]], F32, name=name)
+            copy(dc[:], part)
             return dc
 
         def scatter(window, first, dc):
@@ -181,107 +203,86 @@ def tile_attend_gmla_c_pl_kernel(tc, qT, G, wk, ts, cf, offs, out_0, out_1, out_
             nc.vector.tensor_copy(window[:].indirect(entries), dc[:])
 
         dk_early = stage("dk_early", "dk_early", 2 * K)
-        dk_late = stage("dk_late", "dk_late", 2 * K)
-        w_grouped = [stage("w_grouped%d" % t, "w_grouped%d" % t) for t in range(2)]
+        dk_late = [stage("dk_late0", "dk_late0"), stage("dk_late1", None, offset=1536)]
+        w_early = stage("w_early", "w_early", 2 * K)
         w_late = stage("w_late", "w_late", 2 * K)
 
-        quantise_grad(g_cols(0), g_interleave(0, nc.vector.tensor_copy, "q_paired1"))
-        quantise_grad(g_cols(1), g_interleave(1, nc.scalar.copy, "q_paired3"))
-        b = [first_product(0), first_product(1)]
-        w0 = w_pairs(0, w_raw[0][:], nc.scalar.copy, "q_grouped1")
-        g2 = g_interleave(2, nc.scalar.copy, "q_grouped3")
-        dk = [dk_pairs(0, b[0]), dk_pairs(1, b[1])]
-        turn_words(w0, w_grouped[0][:])
-        turn_words(dk[0], dk_early[:, :K])
-        turn_words(dk[1], dk_early[:, K:])
-        g3 = g_interleave(3, nc.vector.tensor_copy, "dk_paired0")
+        g01 = [g_interleave(0, nc.vector.tensor_copy, "q_paired1"), g_interleave(1, nc.vector.tensor_copy, None, SLOT_B)]
+        quantise_grad(g_cols(0), g01[0])
+        quantise_grad(g_cols(1), g01[1])
+        b = {0: first_product(0), 1: first_product(1)}
+        g2 = g_interleave(2, nc.vector.tensor_copy, None, SLOT_B)
+        quantise_grad(g_cols(3), g_interleave(3, nc.scalar.copy, None, SLOT_A))
         quantise_grad(g_cols(2), g2)
-        w_quantise(0, w_grouped[0])
-        quantise_grad(g_cols(3), g3)
-        b.extend([first_product(2), first_product(3)])
+        windows.append(zeroed_window("window1", None, SLOT_B + 512 - 4 * TOKENS))
+        w01 = w_pairs(0, 2, "q_grouped3")
+        b[3] = first_product(3)
+        turn_words(dk_pairs(0, b[0])[:], dk_early[:, :K])
+        b[2] = first_product(2)
+        turn_words(dk_pairs(1, b[1])[:], dk_early[:, K:])
+        turn_words(w01[:], w_early[:])
+        turn_words(dk_pairs(3, b[3])[:], dk_late[0][:])
+        turn_words(dk_pairs(2, b[2])[:], dk_late[1][:])
         quantise_grad(slice(SLOTS, SLOTS + HALF), dk_early)
-        windows.append(zeroed_window("window1", "dk_early"))
-        w1 = w_pairs(1, w_raw[1][:], nc.vector.tensor_copy, "dk_paired0")
-        w23 = stage("w_paired23", "dk_paired1", 2 * K)
-        nc.scalar.copy(
-            w23[:].rearrange("m (t u p e) -> m t u p e", t=2, u=2, e=2),
-            w_late_raw[:].rearrange("m t (p e u) -> m t u p e", u=2, e=2))
-        early_acc0 = product(0, HALF, 0)
-        dk.extend([dk_pairs(2, b[2]), dk_pairs(3, b[3])])
-        turn_words(w1, w_grouped[1][:])
-        w_quantise(1, w_grouped[1])
-        early0 = copy_out("early0", "dk_paired0", early_acc0[:, HALF:])
-        turn_words(dk[2], dk_late[:, :K])
-        early_acc1 = product(1, HALF, 1)
-        turn_words(dk[3], dk_late[:, K:])
-        turn_words(w23, w_late[:])
-        scatter(windows[0], 0, early0)
-        quantise_grad(slice(SLOTS + HALF, 2 * SLOTS), dk_late)
-        w_quantise(2, w_late)
-        early1 = copy_out("early1", "dk_paired1", early_acc1[:, HALF:])
-        scatter(windows[1], 0, early1)
-        windows.append(zeroed_window("window2", "dk_late"))
-        rest = [
-            copy_out("late0", "late0", product(0, SLOTS, 2)[:, HALF:]),
-            copy_out("late1", "late1", product(1, SLOTS, 3)[:, HALF:]),
-            copy_out("dc2", "dc2", product(2, SLOTS, 0)[:]),
-            copy_out("dc3", "dc3", product(3, SLOTS, 1)[:]),
-        ]
+        w_quantise(0, w_early[:, :K])
+        early_acc = product(0, HALF, 0)
+        w_quantise(1, w_early[:, K:])
+        quantise_grad(slice(SLOTS + 3 * P, SLOTS + 4 * P), dk_late[0])
+        quantise_grad(slice(SLOTS + 2 * P, SLOTS + 3 * P), dk_late[1])
+        windows.append(zeroed_window("window2", None, offset=2048))
+        scatter(windows[0], 0, copy_out("early", nc.vector.tensor_copy, early_acc[:, HALF:]))
+        rest = [copy_out("late", nc.scalar.copy, product(0, SLOTS, 1)[:, HALF:])]
+        turn_words(w_pairs(2, 2, None, offset=0)[:], w_late[:], bank=2)
+        rest.append(copy_out("dc1", nc.scalar.copy, product(1, SLOTS, 2)[:]))
 
         out_rows = out_0.rearrange("(p t) c -> p t c", t=LANES)
-        pairs = [keep.tile([P, 2, CHUNK, 2], BF16, name="pairs%d" % c, align_bytes=64) for c in range(CHUNKS)]
+        words_out = out_1[0].rearrange("p c l -> p (c l)").bitcast(I32)
+        y_scales = keep.tile([P, TOKENS], U8, name="y_scales", align_bytes=64)
+        starts = [sum(CHUNKS[:c]) for c in range(len(CHUNKS))]
+        spent = ["w_codes", "w_scales"]
+        y_grouped = [
+            keep.tile([P, width, LANES], BF16, name="y_grouped%d" % c, tag=spent[c] if c < len(spent) else "y_grouped%d" % c, align_bytes=64)
+            for c, width in enumerate(CHUNKS)]
 
-        def round_lane(engine_copy, t, c):
-            engine_copy(pairs[c][:, t // 2, :, t % 2], windows[t % 3][:, c * CHUNK : (c + 1) * CHUNK])
+        def round_lane(t, cut, left_copy, right_copy):
+            for c, width in (list(enumerate(CHUNKS))[:1] + list(enumerate(CHUNKS))[:0:-1] if t == 0 else enumerate(CHUNKS)):
+                inner = min(max(cut - starts[c], 0), width)
+                pieces = [(left_copy, 0, inner), (right_copy, inner, width)]
+                if t == LANES - 1 and c == len(CHUNKS) - 1:
+                    pieces = [(right_copy, lo, lo + LAST_PIECE) for lo in range(0, width, LAST_PIECE)]
+                for copy, lo, hi in pieces:
+                    if lo == hi:
+                        continue
+                    src = windows[t % 3][:, starts[c] + lo : starts[c] + hi]
+                    if t == 2:
+                        copy(y_grouped[c][:, lo:hi, 2:4], src.unsqueeze(2).to_broadcast([P, hi - lo, 2]))
+                    else:
+                        copy(y_grouped[c][:, lo:hi, t], src)
 
-        def round_both(engine_copy, c):
-            engine_copy(pairs[c][:, 1], windows[2][:, c * CHUNK : (c + 1) * CHUNK].unsqueeze(2).to_broadcast([P, CHUNK, 2]))
-
-        def gpsimd_round(out, in_):
-            nc.gpsimd.tensor_scalar(out=out, in0=in_, scalar1=1.0, scalar2=0.0, op0=MULT, op1=ADD)
+        def quantise(c):
+            y_codes = keep.tile([P, CHUNKS[c]], U32, name="y_codes%d" % c, align_bytes=64)
+            step = LAST_PIECE if c == len(CHUNKS) - 1 else CHUNKS[c]
+            for lo in range(0, CHUNKS[c], step):
+                nc.vector.quantize_mx(
+                    out=y_codes[:, lo : lo + step].bitcast(E4M3), scales=y_scales[:, starts[c] + lo : starts[c] + lo + step],
+                    in_=y_grouped[c][:, lo : lo + step, :].rearrange("p c t -> p (c t)"))
+            nc.sync.dma_start(words_out[:, starts[c] : starts[c] + CHUNKS[c]], y_codes[:].bitcast(I32))
 
         for t in range(LANES):
             window = windows[t % 3]
             scatter(window, SLOTS - rest[t].shape[1], rest[t])
             nc.sync.dma_start(out_rows[:, t, :], window[:])
-            if t < 2:
-                for c in range(CHUNKS):
-                    round_lane(nc.scalar.copy if c < 2 else gpsimd_round, t, c)
-            if t == 2:
-                round_both(nc.scalar.copy, 0)
-                round_both(gpsimd_round, CHUNKS - 1)
-                for c in range(1, CHUNKS - 1):
-                    round_lane(nc.scalar.copy, t, c)
+            if t == 0:
+                w_quantise(2, w_late[:])
+                for lane, bank in ((2, 3), (3, 0)):
+                    rest.append(copy_out("dc%d" % lane, nc.scalar.copy, product(lane, SLOTS, bank)[:]))
+            if t < LANES - 1:
+                round_lane(t, SCALAR_EARLY, nc.scalar.copy, gpsimd_round)
 
-        last = LANES - 1
-        words_out = out_1[0].rearrange("p c l -> p (c l)").bitcast(I32)
-        y_scales = keep.tile([P, TOKENS], U8, name="y_scales", align_bytes=64)
-        y_grouped = [keep.tile([P, CHUNK * LANES], BF16, name="y_grouped%d" % c, align_bytes=64) for c in range(CHUNKS)]
-
-        def merge(engine_copy, c):
-            engine_copy(
-                y_grouped[c][:].bitcast(F32).rearrange("p (c u) -> p c u", u=2),
-                pairs[c][:].rearrange("p u c e -> p (u c e)").bitcast(F32).rearrange("p (u c) -> p c u", u=2),
-            )
-
-        def quantise(c):
-            cols = slice(c * CHUNK, (c + 1) * CHUNK)
-            y_codes = keep.tile([P, CHUNK], U32, name="y_codes%d" % c, align_bytes=64)
-            nc.vector.quantize_mx(out=y_codes[:].bitcast(E4M3), scales=y_scales[:, cols], in_=y_grouped[c][:])
-            nc.sync.dma_start(words_out[:, cols], y_codes[:].bitcast(I32))
-
-        round_lane(nc.vector.tensor_copy, last, 0)
-        for c in range(1, CHUNKS):
-            round_lane(nc.scalar.copy, last, c)
-        merge(nc.scalar.copy, CHUNKS - 1)
-        merge(nc.vector.tensor_copy, 0)
-        merge(nc.vector.tensor_copy, 1)
-        quantise(0)
-        merge(nc.vector.tensor_copy, 2)
-        for c in range(1, CHUNKS):
+        round_lane(LANES - 1, VECTOR_LAST, nc.vector.tensor_copy, nc.scalar.copy)
+        for c in range(len(CHUNKS)):
             quantise(c)
         for quad in range(4):
-            queue = nc.sync if quad % 2 == 0 else nc.scalar
-            queue.dma_start(
+            nc.sync.dma_start(
                 out_2[0, 4 * quad : 4 * quad + 4, :].bitcast(I32),
                 y_scales[32 * quad : 32 * quad + 4, :].bitcast(I32))

@@ -20,12 +20,13 @@ K = 512
 SLOTS = 512
 TILES = SLOTS // P
 TOKENS = 2048
-CHUNKS = [512, 512, 512, 512]
+CHUNK = 512
+CHUNKS = TOKENS // CHUNK
+DIRECT = 2
 LAST_PIECE = 256
+VECTOR_LAST = 928
 SLOT_A = 18432
 SLOT_B = SLOT_A + 1024
-SCALAR_EARLY = 832
-VECTOR_LAST = 896
 HALF = SLOTS // 2
 TS_ROW = P - 1
 
@@ -238,35 +239,26 @@ def tile_attend_gmla_c_pl_kernel(tc, qT, G, wk, ts, cf, offs, out_0, out_1, out_
         out_rows = out_0.rearrange("(p t) c -> p t c", t=LANES)
         words_out = out_1[0].rearrange("p c l -> p (c l)").bitcast(I32)
         y_scales = keep.tile([P, TOKENS], U8, name="y_scales", align_bytes=64)
-        starts = [sum(CHUNKS[:c]) for c in range(len(CHUNKS))]
-        spent = ["w_codes", "w_scales"]
-        y_grouped = [
-            keep.tile([P, width, LANES], BF16, name="y_grouped%d" % c, tag=spent[c] if c < len(spent) else "y_grouped%d" % c, align_bytes=64)
-            for c, width in enumerate(CHUNKS)]
+        spent = ["w_codes", "y_grouped1", "y_grouped2", "y_grouped3"]
+        y_grouped = [keep.tile([P, CHUNK, LANES], BF16, name="y_grouped%d" % c, tag=spent[c], align_bytes=64) for c in range(CHUNKS)]
+        pairs = {
+            2: keep.tile([P, 2, CHUNK, 2], BF16, name="pairs2", tag="w_scales", align_bytes=64),
+            3: keep.tile([P, 2, CHUNK, 2], BF16, name="pairs3", align_bytes=64),
+        }
 
-        def round_lane(t, cut, left_copy, right_copy):
-            for c, width in (list(enumerate(CHUNKS))[:1] + list(enumerate(CHUNKS))[:0:-1] if t == 0 else enumerate(CHUNKS)):
-                inner = min(max(cut - starts[c], 0), width)
-                pieces = [(left_copy, 0, inner), (right_copy, inner, width)]
-                if t == LANES - 1 and c == len(CHUNKS) - 1:
-                    pieces = [(right_copy, lo, lo + LAST_PIECE) for lo in range(0, width, LAST_PIECE)]
-                for copy, lo, hi in pieces:
-                    if lo == hi:
-                        continue
-                    src = windows[t % 3][:, starts[c] + lo : starts[c] + hi]
-                    if t == 2:
-                        copy(y_grouped[c][:, lo:hi, 2:4], src.unsqueeze(2).to_broadcast([P, hi - lo, 2]))
-                    else:
-                        copy(y_grouped[c][:, lo:hi, t], src)
+        def round_lane(copy, t, c, lo=0, hi=CHUNK, both=False):
+            src = windows[t % 3][:, c * CHUNK + lo : c * CHUNK + hi]
+            word = y_grouped[c][:, lo:hi, t // 2 * 2 : t // 2 * 2 + 2] if c < DIRECT else pairs[c][:, t // 2, lo:hi, :]
+            if both:
+                copy(word, src.unsqueeze(2).to_broadcast([P, hi - lo, 2]))
+            else:
+                copy(word[:, :, t % 2], src)
 
-        def quantise(c):
-            y_codes = keep.tile([P, CHUNKS[c]], U32, name="y_codes%d" % c, align_bytes=64)
-            step = LAST_PIECE if c == len(CHUNKS) - 1 else CHUNKS[c]
-            for lo in range(0, CHUNKS[c], step):
-                nc.vector.quantize_mx(
-                    out=y_codes[:, lo : lo + step].bitcast(E4M3), scales=y_scales[:, starts[c] + lo : starts[c] + lo + step],
-                    in_=y_grouped[c][:, lo : lo + step, :].rearrange("p c t -> p (c t)"))
-            nc.sync.dma_start(words_out[:, starts[c] : starts[c] + CHUNKS[c]], y_codes[:].bitcast(I32))
+        def merge(c, lo, hi):
+            nc.scalar.copy(
+                y_grouped[c][:, lo:hi, :].rearrange("p c t -> p (c t)").bitcast(F32).rearrange("p (c u) -> p c u", u=2),
+                pairs[c][:].rearrange("p u c e -> p (u c e)").bitcast(F32).rearrange("p (u c) -> p c u", u=2)[:, lo:hi, :],
+            )
 
         for t in range(LANES):
             window = windows[t % 3]
@@ -277,12 +269,31 @@ def tile_attend_gmla_c_pl_kernel(tc, qT, G, wk, ts, cf, offs, out_0, out_1, out_
                 for lane, bank in ((2, 3), (3, 0)):
                     rest.append(copy_out("dc%d" % lane, nc.scalar.copy, product(lane, SLOTS, bank)[:]))
             if t < LANES - 1:
-                round_lane(t, SCALAR_EARLY, nc.scalar.copy, gpsimd_round)
+                for c in range(CHUNKS):
+                    round_lane(nc.scalar.copy if c % 2 == 0 else gpsimd_round, t, c, both=(t == 2 and c != 2))
 
-        round_lane(LANES - 1, VECTOR_LAST, nc.vector.tensor_copy, nc.scalar.copy)
-        for c in range(len(CHUNKS)):
-            quantise(c)
+        last = LANES - 1
+        for c in range(CHUNKS):
+            step = LAST_PIECE if c == CHUNKS - 1 else CHUNK
+            if c < DIRECT:
+                cut = min(VECTOR_LAST - c * CHUNK, CHUNK)
+                round_lane(nc.vector.tensor_copy, last, c, 0, cut)
+                if cut < CHUNK:
+                    round_lane(nc.scalar.copy, last, c, cut, CHUNK)
+            else:
+                round_lane(nc.scalar.copy, last, c)
+                for lo in range(0, CHUNK, step):
+                    merge(c, lo, lo + step)
+        for c in range(CHUNKS):
+            step = LAST_PIECE if c == CHUNKS - 1 else CHUNK
+            y_codes = keep.tile([P, CHUNK], U32, name="y_codes%d" % c, align_bytes=64)
+            for lo in range(0, CHUNK, step):
+                nc.vector.quantize_mx(
+                    out=y_codes[:, lo : lo + step].bitcast(E4M3), scales=y_scales[:, c * CHUNK + lo : c * CHUNK + lo + step],
+                    in_=y_grouped[c][:, lo : lo + step, :].rearrange("p c t -> p (c t)"))
+            nc.sync.dma_start(words_out[:, c * CHUNK : (c + 1) * CHUNK], y_codes[:].bitcast(I32))
         for quad in range(4):
-            nc.sync.dma_start(
+            queue = nc.sync if quad % 2 == 0 else nc.scalar
+            queue.dma_start(
                 out_2[0, 4 * quad : 4 * quad + 4, :].bitcast(I32),
                 y_scales[32 * quad : 32 * quad + 4, :].bitcast(I32))

@@ -22,11 +22,13 @@ TILES = SLOTS // P
 TOKENS = 2048
 CHUNK = 512
 CHUNKS = TOKENS // CHUNK
-DIRECT = 2
+DIRECT = 3
+SCALAR_DIRECT = 832
 LAST_PIECE = 256
-VECTOR_LAST = 928
+VECTOR_LAST = 1120
 SLOT_A = 18432
 SLOT_B = SLOT_A + 1024
+SLOT_C = SLOT_B + 2048
 HALF = SLOTS // 2
 TS_ROW = P - 1
 
@@ -124,7 +126,7 @@ def tile_attend_gmla_c_pl_kernel(tc, qT, G, wk, ts, cf, offs, out_0, out_1, out_
             cols = slice(t * P, (t + 1) * P)
             paired = stage("q_paired%d" % t, "q_paired%d" % t, offset=SLOT_B if t == 3 else None)
             round_pairs(round_copy, q_raw[h][u], "m (p u e) -> m u p e", paired)
-            grouped = stage("q_grouped%d" % t, "q_grouped%d" % t, offset=SLOT_A if t == 1 else None)
+            grouped = stage("q_grouped%d" % t, "q_grouped%d" % t, offset={1: SLOT_A, 3: SLOT_C}.get(t))
             turn_words(paired[:], grouped[:])
             nc.vector.quantize_mx(out=q_codes[:, cols].bitcast(E4M3), scales=q_scales[:, cols], in_=grouped[:])
 
@@ -194,8 +196,11 @@ def tile_attend_gmla_c_pl_kernel(tc, qT, G, wk, ts, cf, offs, out_0, out_1, out_
                 rhs=grad_codes[:, moving].bitcast(E5M2), rhs_scale=grad_scales[:, moving], start=True, stop=True)
             return acc
 
-        def copy_out(name, copy, part):
-            dc = keep.tile([P, part.shape[1]], F32, name=name)
+        def copy_out(name, copy, part, offset=None):
+            if offset is None:
+                dc = keep.tile([P, part.shape[1]], F32, name=name)
+            else:
+                dc = placed.tile([P, part.shape[1]], F32, name=name, offset=offset, align_bytes=64)
             copy(dc[:], part)
             return dc
 
@@ -204,8 +209,8 @@ def tile_attend_gmla_c_pl_kernel(tc, qT, G, wk, ts, cf, offs, out_0, out_1, out_
             nc.vector.tensor_copy(window[:].indirect(entries), dc[:])
 
         dk_early = stage("dk_early", "dk_early", 2 * K)
-        dk_late = [stage("dk_late0", "dk_late0"), stage("dk_late1", None, offset=1536)]
-        w_early = stage("w_early", "w_early", 2 * K)
+        dk_late = [stage("dk_late0", None, offset=0), stage("dk_late1", None, offset=3072)]
+        w_early = [stage("w_early%d" % t, "w_early%d" % t) for t in range(2)]
         w_late = stage("w_late", "w_late", 2 * K)
 
         g01 = [g_interleave(0, nc.vector.tensor_copy, "q_paired1"), g_interleave(1, nc.vector.tensor_copy, None, SLOT_B)]
@@ -216,35 +221,38 @@ def tile_attend_gmla_c_pl_kernel(tc, qT, G, wk, ts, cf, offs, out_0, out_1, out_
         quantise_grad(g_cols(3), g_interleave(3, nc.scalar.copy, None, SLOT_A))
         quantise_grad(g_cols(2), g2)
         windows.append(zeroed_window("window1", None, SLOT_B + 512 - 4 * TOKENS))
-        w01 = w_pairs(0, 2, "q_grouped3")
+        w01 = [w_pairs(t, 1, None, SLOT_C - 512 + 1024 * t) for t in range(2)]
         b[3] = first_product(3)
+        turn_words(w01[0][:], w_early[0][:])
         turn_words(dk_pairs(0, b[0])[:], dk_early[:, :K])
         b[2] = first_product(2)
         turn_words(dk_pairs(1, b[1])[:], dk_early[:, K:])
-        turn_words(w01[:], w_early[:])
         turn_words(dk_pairs(3, b[3])[:], dk_late[0][:])
+        turn_words(w01[1][:], w_early[1][:])
         turn_words(dk_pairs(2, b[2])[:], dk_late[1][:])
+        w_quantise(0, w_early[0][:])
         quantise_grad(slice(SLOTS, SLOTS + HALF), dk_early)
-        w_quantise(0, w_early[:, :K])
         early_acc = product(0, HALF, 0)
-        w_quantise(1, w_early[:, K:])
         quantise_grad(slice(SLOTS + 3 * P, SLOTS + 4 * P), dk_late[0])
+        w_quantise(1, w_early[1][:])
         quantise_grad(slice(SLOTS + 2 * P, SLOTS + 3 * P), dk_late[1])
-        windows.append(zeroed_window("window2", None, offset=2048))
-        scatter(windows[0], 0, copy_out("early", nc.vector.tensor_copy, early_acc[:, HALF:]))
-        rest = [copy_out("late", nc.scalar.copy, product(0, SLOTS, 1)[:, HALF:])]
-        turn_words(w_pairs(2, 2, None, offset=0)[:], w_late[:], bank=2)
-        rest.append(copy_out("dc1", nc.scalar.copy, product(1, SLOTS, 2)[:]))
+        scatter(windows[0], 0, copy_out("early", nc.vector.tensor_copy, early_acc[:, HALF:], 3072))
+        late_acc = product(0, SLOTS, 1)
+        w23 = w_pairs(2, 2, None, offset=0)
+        turn_words(w23[:, :K], w_late[:, :K])
+        turn_words(w23[:, K:], w_late[:, K:])
+        w_quantise(2, w_late[:])
+        windows.append(zeroed_window("window2", "w_late"))
+        rest = [copy_out("late", nc.scalar.copy, late_acc[:, HALF:], 0), copy_out("dc1", nc.scalar.copy, product(1, SLOTS, 2)[:], 1024)]
+        for lane, bank in ((2, 3), (3, 0)):
+            rest.append(copy_out("dc%d" % lane, nc.scalar.copy, product(lane, SLOTS, bank)[:]))
 
         out_rows = out_0.rearrange("(p t) c -> p t c", t=LANES)
         words_out = out_1[0].rearrange("p c l -> p (c l)").bitcast(I32)
         y_scales = keep.tile([P, TOKENS], U8, name="y_scales", align_bytes=64)
-        spent = ["w_codes", "y_grouped1", "y_grouped2", "y_grouped3"]
+        spent = ["w_codes", "w_scales", "y_grouped2", "y_grouped3"]
         y_grouped = [keep.tile([P, CHUNK, LANES], BF16, name="y_grouped%d" % c, tag=spent[c], align_bytes=64) for c in range(CHUNKS)]
-        pairs = {
-            2: keep.tile([P, 2, CHUNK, 2], BF16, name="pairs2", tag="w_scales", align_bytes=64),
-            3: keep.tile([P, 2, CHUNK, 2], BF16, name="pairs3", align_bytes=64),
-        }
+        pairs = {3: keep.tile([P, 2, CHUNK, 2], BF16, name="pairs3", tag="grad_scales", align_bytes=64)}
 
         def round_lane(copy, t, c, lo=0, hi=CHUNK, both=False):
             src = windows[t % 3][:, c * CHUNK + lo : c * CHUNK + hi]
@@ -264,20 +272,23 @@ def tile_attend_gmla_c_pl_kernel(tc, qT, G, wk, ts, cf, offs, out_0, out_1, out_
             window = windows[t % 3]
             scatter(window, SLOTS - rest[t].shape[1], rest[t])
             nc.sync.dma_start(out_rows[:, t, :], window[:])
-            if t == 0:
-                w_quantise(2, w_late[:])
-                for lane, bank in ((2, 3), (3, 0)):
-                    rest.append(copy_out("dc%d" % lane, nc.scalar.copy, product(lane, SLOTS, bank)[:]))
             if t < LANES - 1:
-                for c in range(CHUNKS):
-                    round_lane(nc.scalar.copy if c % 2 == 0 else gpsimd_round, t, c, both=(t == 2 and c != 2))
+                for c in range(DIRECT):
+                    cut = min(max(SCALAR_DIRECT - c * CHUNK, 0), CHUNK)
+                    if cut > 0:
+                        round_lane(nc.scalar.copy, t, c, 0, cut, both=(t == 2))
+                    if cut < CHUNK:
+                        round_lane(gpsimd_round, t, c, cut, CHUNK, both=(t == 2))
+                round_lane(nc.scalar.copy, t, DIRECT, 0, CHUNK // 2)
+                round_lane(gpsimd_round, t, DIRECT, CHUNK // 2, CHUNK, both=(t == 2))
 
         last = LANES - 1
         for c in range(CHUNKS):
             step = LAST_PIECE if c == CHUNKS - 1 else CHUNK
             if c < DIRECT:
-                cut = min(VECTOR_LAST - c * CHUNK, CHUNK)
-                round_lane(nc.vector.tensor_copy, last, c, 0, cut)
+                cut = min(max(VECTOR_LAST - c * CHUNK, 0), CHUNK)
+                if cut > 0:
+                    round_lane(nc.vector.tensor_copy, last, c, 0, cut)
                 if cut < CHUNK:
                     round_lane(nc.scalar.copy, last, c, cut, CHUNK)
             else:

@@ -79,7 +79,8 @@ def tile_attend_gmla_c_pl_kernel(tc, qT, G, wk, ts, cf, offs, out_0, out_1, out_
             nc.gpsimd.memset(window[:].bitcast(I32), 0)
             return window
 
-        windows = [zeroed_window("window0", "window0")]
+        windows = [keep.tile([P, TOKENS], F32, name="window0")]
+        nc.vector.memset(windows[0][:].bitcast(I32), 0)
 
         def stage(name, tag, width=K, offset=None):
             if offset is None:

@@ -13,6 +13,7 @@ E4M3 = mybir.dt.float8_e4m3fn_x4
 E5M2 = mybir.dt.float8_e5m2_x4
 MULT = mybir.AluOpType.mult
 ADD = mybir.AluOpType.add
+COPY = mybir.ActivationFunctionType.Copy
 
 P = 128
 LANES = 4
@@ -22,15 +23,9 @@ TILES = SLOTS // P
 TOKENS = 2048
 CHUNK = 512
 CHUNKS = TOKENS // CHUNK
-DIRECT = 3
-SCALAR_DIRECT = 832
-LAST_PIECE = 256
-VECTOR_LAST = 1120
-SLOT_A = 18432
-SLOT_B = SLOT_A + 1024
-SLOT_C = SLOT_B + 2048
 HALF = SLOTS // 2
 TS_ROW = P - 1
+KB = 1024
 
 FLOPS = 2 * 2 * 512 * 512 * 512
 
@@ -43,13 +38,20 @@ def tile_attend_gmla_c_pl_kernel(tc, qT, G, wk, ts, cf, offs, out_0, out_1, out_
         turn = ctx.enter_context(tc.psum_pool(name="turn", bufs=4))
         placed = ctx.enter_context(tc.tile_pool(name="placed", bufs=1))
 
+        def sbuf(name, shape, dtype, offset=None):
+            if offset is None:
+                return keep.tile(shape, dtype, name=name, align_bytes=64)
+            return placed.tile(shape, dtype, name=name, offset=offset, align_bytes=64)
+
         q_rows = qT.rearrange("(h m u) r -> h m u r", h=2, u=2)
         w_rows = wk.rearrange("(m t) f -> m t f", t=LANES)
         g_rows = G.rearrange("(p j) i -> p j i", j=LANES)
         q_first = keep.tile([P, 2, K], F32, name="q_first")
         q_second = [keep.tile([P, K], F32, name="q_second%d" % u) for u in range(2)]
         q_raw = [[q_first[:, u, :] for u in range(2)], [q_second[u][:] for u in range(2)]]
-        w_raw = [keep.tile([P, 2, K], F32, name="w_raw%d" % h) for h in range(2)]
+        w_first = keep.tile([P, 1, K], F32, name="w_first")
+        w_second = keep.tile([P, 1, K], F32, name="w_second")
+        w_last = keep.tile([P, 2, K], F32, name="w_last")
         g_raw = [keep.tile([P, LANES, HALF], F32, name="g_raw%d" % h) for h in range(2)]
         offsets = keep.tile([P, SLOTS // 16], U16, name="offsets")
         ts_window = keep.tile([P, TOKENS], F32, name="ts_window")
@@ -63,34 +65,32 @@ def tile_attend_gmla_c_pl_kernel(tc, qT, G, wk, ts, cf, offs, out_0, out_1, out_
             nc.sync.dma_start(q_raw[1][u], q_rows[1, :, u, :])
         nc.sync.dma_start(g_raw[0][:], g_rows[:, :, :HALF])
         nc.sync.dma_start(g_raw[1][:], g_rows[:, :, HALF:])
-        nc.sync.dma_start(w_raw[0][:], w_rows[:, :2, :])
-        nc.sync.dma_start(w_raw[1][:], w_rows[:, 2:, :])
+        nc.sync.dma_start(w_first[:], w_rows[:, 0:1, :])
+        nc.sync.dma_start(w_second[:], w_rows[:, 1:2, :])
+        nc.sync.dma_start(w_last[:], w_rows[:, 2:, :])
 
         ident = keep.tile([P, P], F32, name="ident")
         make_identity(nc, ident[:])
 
-        nc.vector.memset(ts_window[0:TS_ROW, :].bitcast(I32), 0)
+        def zero_one_port(part):
+            width = part.shape[1]
+            nc.vector.memset(part[:, : width - 1].bitcast(I32), 0)
+            nc.vector.memset(part[:, width - 1 :].bitcast(I32), 0)
 
-        def zeroed_window(name, tag, offset=None):
-            if offset is None:
-                window = keep.tile([P, TOKENS], F32, name=name, tag=tag, align_bytes=64)
-            else:
-                window = placed.tile([P, TOKENS], F32, name=name, offset=offset, align_bytes=64)
-            nc.gpsimd.memset(window[:].bitcast(I32), 0)
-            return window
+        zero_one_port(ts_window[0:TS_ROW, :])
+        window_a = sbuf("window_a", [P, TOKENS], F32)
+        nc.gpsimd.memset(window_a[:].bitcast(I32), 0)
 
-        windows = [keep.tile([P, TOKENS], F32, name="window0")]
-        nc.vector.memset(windows[0][:].bitcast(I32), 0)
+        ts_row = keep.tile([P, SLOTS], F32, name="ts_row")
+        nc.vector.tensor_copy(ts_row[:], ts_window[:].indirect(offsets[:]))
 
-        def stage(name, tag, width=K, offset=None):
-            if offset is None:
-                return keep.tile([P, width], BF16, name=name, tag=tag, align_bytes=64)
-            return placed.tile([P, width], BF16, name=name, offset=offset, align_bytes=64)
+        window_b = sbuf("window_b", [P, TOKENS], F32)
+        nc.gpsimd.memset(window_b[:].bitcast(I32), 0)
 
         def round_pairs(round_copy, raw, order, paired):
             round_copy(paired[:].rearrange("m (u p e) -> m u p e", u=2, e=2), raw.rearrange(order, u=2, e=2))
 
-        def turn_words(paired, grouped, bank=None):
+        def turn_words(paired, grouped, copy, bank=None):
             words = paired.bitcast(F32)
             blocks = words.shape[1] // P
             if bank is None:
@@ -99,13 +99,10 @@ def tile_attend_gmla_c_pl_kernel(tc, qT, G, wk, ts, cf, offs, out_0, out_1, out_
                 turned = psum.tile([P, blocks, P], F32, name="acc%d" % bank)
             for block in range(blocks):
                 nc.tensor.transpose(turned[:, block, :], words[:, block * P : (block + 1) * P], ident[:])
-            nc.scalar.copy(
+            copy(
                 grouped.bitcast(F32).rearrange("p (t m u) -> p t m u", m=P, u=2),
                 turned[:].rearrange("p (t u) m -> p t m u", u=2),
             )
-
-        ts_row = keep.tile([P, SLOTS], F32, name="ts_row")
-        nc.vector.tensor_copy(ts_row[:], ts_window[:].indirect(offsets[:]))
 
         cf_wide = keep.tile([P, LANES, P], F32, name="cf_wide")
         nc.scalar.copy(cf_wide[:], cf_cols[:].unsqueeze(2).to_broadcast([P, LANES, P]))
@@ -119,16 +116,23 @@ def tile_attend_gmla_c_pl_kernel(tc, qT, G, wk, ts, cf, offs, out_0, out_1, out_
             cf_turned[:].rearrange("i (e u) p -> i u p e", u=2),
         )
 
-        q_codes = keep.tile([P, K], U32, name="q_codes", align_bytes=64)
-        q_scales = keep.tile([P, K], U8, name="q_scales", align_bytes=64)
+        q_codes = sbuf("q_codes", [P, K], U32)
+        q_scales = sbuf("q_scales", [P, K], U8)
+
+        AT_QG1, AT_QP3, AT_QG3 = 0, 1 * KB, 2 * KB
+        AT_GC0 = 4 * KB
+        AT_DK_LATE = 5 * KB
+        AT_W23 = 16 * KB
+        AT_DC2 = 28 * KB
+        AT_DC3 = 40 * KB
 
         def q_operand(h, u, round_copy):
             t = 2 * u + h
             cols = slice(t * P, (t + 1) * P)
-            paired = stage("q_paired%d" % t, "q_paired%d" % t, offset=SLOT_B if t == 3 else None)
+            paired = sbuf("q_paired%d" % t, [P, K], BF16, {3: AT_QP3}.get(t))
             round_pairs(round_copy, q_raw[h][u], "m (p u e) -> m u p e", paired)
-            grouped = stage("q_grouped%d" % t, "q_grouped%d" % t, offset={1: SLOT_A, 3: SLOT_C}.get(t))
-            turn_words(paired[:], grouped[:])
+            grouped = sbuf("q_grouped%d" % t, [P, K], BF16, {1: AT_QG1, 3: AT_QG3}.get(t))
+            turn_words(paired[:], grouped[:], nc.scalar.copy)
             nc.vector.quantize_mx(out=q_codes[:, cols].bitcast(E4M3), scales=q_scales[:, cols], in_=grouped[:])
 
         q_operand(0, 0, nc.scalar.copy)
@@ -143,166 +147,186 @@ def tile_attend_gmla_c_pl_kernel(tc, qT, G, wk, ts, cf, offs, out_0, out_1, out_
         q_operand(1, 0, nc.vector.tensor_copy)
         q_operand(1, 1, nc.vector.tensor_copy)
 
-        grad_codes = keep.tile([P, 2 * SLOTS], U32, name="grad_codes", align_bytes=64)
-        grad_scales = keep.tile([P, 2 * SLOTS], U8, name="grad_scales", align_bytes=64)
-        w_codes = keep.tile([P, K], U32, name="w_codes", align_bytes=64)
-        w_scales = keep.tile([P, K], U8, name="w_scales", align_bytes=64)
-
-        def g_cols(s):
-            return slice((s + 2) % TILES * P, ((s + 2) % TILES + 1) * P)
-
-        def quantise_grad(cols, grouped):
-            nc.vector.quantize_mx(out=grad_codes[:, cols].bitcast(E5M2), scales=grad_scales[:, cols], in_=grouped[:])
+        dk_codes = sbuf("dk_codes", [P, SLOTS], U32)
+        dk_scales = sbuf("dk_scales", [P, SLOTS], U8)
+        w_codes = sbuf("w_codes", [P, K], U32)
+        w_scales = sbuf("w_scales", [P, K], U8)
 
         def gpsimd_round(out, in_):
             nc.gpsimd.tensor_scalar(out=out, in0=in_, scalar1=1.0, scalar2=0.0, op0=MULT, op1=ADD)
 
-        def g_interleave(s, copy, tag, offset=None):
-            grouped = stage("g_grouped%d" % s, tag, offset=offset)
+        def g_interleave(s, copy, grouped):
             src = g_raw[s // 2][:, :, (s % 2) * P : (s % 2 + 1) * P]
-            copy(grouped[:].rearrange("p (c i t) -> p c t i", i=4, t=LANES), src.rearrange("p t (c i) -> p c t i", i=4))
-            return grouped
+            copy(grouped.rearrange("p (c i t) -> p c t i", i=4, t=LANES), src.rearrange("p t (c i) -> p c t i", i=4))
 
-        def first_product(s):
+        def first_product(s, codes, scales):
             acc = psum.tile([P, K], F32, name="acc%d" % s)
             nc.tensor.matmul_mx(
-                out=acc[:], lhsT=grad_codes[:, g_cols(s)].bitcast(E5M2), lhsT_scale=grad_scales[:, g_cols(s)],
+                out=acc[:], lhsT=codes.bitcast(E5M2), lhsT_scale=scales,
                 rhs=q_codes[:].bitcast(E4M3), rhs_scale=q_scales[:], start=True, stop=True)
             return acc
 
         def dk_pairs(s, acc):
-            paired = stage("dk_paired%d" % s, "dk_paired%d" % s, offset=SLOT_B + 512 if s == 0 else None)
+            paired = sbuf("dk_paired%d" % s, [P, K], BF16)
             nc.vector.scalar_tensor_tensor(
                 out=paired[:], in0=acc[:], scalar=ts_cols[:, s : s + 1], in1=cf_all[:], op0=MULT, op1=MULT)
             return paired
 
-        def w_pairs(first, count, tag, offset=None):
-            paired = stage("w_paired%d" % first, tag, count * K, offset)
-            raw = w_raw[first // 2][:, first % 2 : first % 2 + count, :]
-            nc.scalar.copy(
-                paired[:].rearrange("m (t u p e) -> m t u p e", t=count, u=2, e=2),
-                raw.rearrange("m t (p e u) -> m t u p e", u=2, e=2))
+        def quantise_dk(first, grouped):
+            cols = slice(first, first + grouped.shape[1] // LANES)
+            nc.vector.quantize_mx(out=dk_codes[:, cols].bitcast(E5M2), scales=dk_scales[:, cols], in_=grouped)
+
+        def w_pairs(name, round_copy, raw, offset):
+            paired = sbuf(name, [P, K], BF16, offset)
+            round_pairs(round_copy, raw, "m (p e u) -> m u p e", paired)
             return paired
 
-        def w_quantise(first, grouped):
-            cols = slice(first * P, first * P + grouped.shape[1] // LANES)
+        def w_quantise(lane, grouped):
+            cols = slice(lane * P, lane * P + grouped.shape[1] // LANES)
             nc.vector.quantize_mx(out=w_codes[:, cols].bitcast(E4M3), scales=w_scales[:, cols], in_=grouped)
 
-        def product(t, first, bank):
-            cols = slice(t * P, (t + 1) * P)
-            moving = slice(first, first + SLOTS)
-            acc = psum.tile([P, SLOTS], F32, name="acc%d" % bank)
+        def product(lane, first, count, bank):
+            cols = slice(lane * P, (lane + 1) * P)
+            moving = slice(first, first + count)
+            acc = psum.tile([P, count], F32, name="acc%d" % bank)
             nc.tensor.matmul_mx(
                 out=acc[:], lhsT=w_codes[:, cols].bitcast(E4M3), lhsT_scale=w_scales[:, cols],
-                rhs=grad_codes[:, moving].bitcast(E5M2), rhs_scale=grad_scales[:, moving], start=True, stop=True)
+                rhs=dk_codes[:, moving].bitcast(E5M2), rhs_scale=dk_scales[:, moving], start=True, stop=True)
             return acc
 
-        def copy_out(name, copy, part, offset=None):
-            if offset is None:
-                dc = keep.tile([P, part.shape[1]], F32, name=name)
-            else:
-                dc = placed.tile([P, part.shape[1]], F32, name=name, offset=offset, align_bytes=64)
-            copy(dc[:], part)
+        def copy_out(name, copy, acc, offset=None):
+            dc = sbuf(name, [P, acc.shape[1]], F32, offset)
+            copy(dc[:], acc[:])
             return dc
 
-        def scatter(window, first, dc):
-            entries = offsets[:, first // 16 : (first + dc.shape[1]) // 16]
-            nc.vector.tensor_copy(window[:].indirect(entries), dc[:])
+        def entries(first, count):
+            return offsets[:, first // 16 : (first + count) // 16]
 
-        dk_early = stage("dk_early", "dk_early", 2 * K)
-        dk_late = [stage("dk_late0", None, offset=0), stage("dk_late1", None, offset=3072)]
-        w_early = [stage("w_early%d" % t, "w_early%d" % t) for t in range(2)]
-        w_late = stage("w_late", "w_late", 2 * K)
+        def vector_scatter(window, first, dc):
+            nc.vector.tensor_copy(window[:].indirect(entries(first, dc.shape[1])), dc)
 
-        g01 = [g_interleave(0, nc.vector.tensor_copy, "q_paired1"), g_interleave(1, nc.vector.tensor_copy, None, SLOT_B)]
-        quantise_grad(g_cols(0), g01[0])
-        quantise_grad(g_cols(1), g01[1])
-        b = {0: first_product(0), 1: first_product(1)}
-        g2 = g_interleave(2, nc.vector.tensor_copy, None, SLOT_B)
-        quantise_grad(g_cols(3), g_interleave(3, nc.scalar.copy, None, SLOT_A))
-        quantise_grad(g_cols(2), g2)
-        windows.append(zeroed_window("window1", None, SLOT_B + 512 - 4 * TOKENS))
-        w01 = [w_pairs(t, 1, None, SLOT_C - 512 + 1024 * t) for t in range(2)]
-        b[3] = first_product(3)
-        turn_words(w01[0][:], w_early[0][:])
-        turn_words(dk_pairs(0, b[0])[:], dk_early[:, :K])
-        b[2] = first_product(2)
-        turn_words(dk_pairs(1, b[1])[:], dk_early[:, K:])
-        turn_words(dk_pairs(3, b[3])[:], dk_late[0][:])
-        turn_words(w01[1][:], w_early[1][:])
-        turn_words(dk_pairs(2, b[2])[:], dk_late[1][:])
-        w_quantise(0, w_early[0][:])
-        quantise_grad(slice(SLOTS, SLOTS + HALF), dk_early)
-        early_acc = product(0, HALF, 0)
-        quantise_grad(slice(SLOTS + 3 * P, SLOTS + 4 * P), dk_late[0])
-        w_quantise(1, w_early[1][:])
-        quantise_grad(slice(SLOTS + 2 * P, SLOTS + 3 * P), dk_late[1])
-        scatter(windows[0], 0, copy_out("early", nc.vector.tensor_copy, early_acc[:, HALF:], 3072))
-        late_acc = product(0, SLOTS, 1)
-        w23 = w_pairs(2, 2, None, offset=0)
-        turn_words(w23[:, :K], w_late[:, :K])
-        turn_words(w23[:, K:], w_late[:, K:])
-        w_quantise(2, w_late[:])
-        windows.append(zeroed_window("window2", "w_late"))
-        rest = [copy_out("late", nc.scalar.copy, late_acc[:, HALF:], 0), copy_out("dc1", nc.scalar.copy, product(1, SLOTS, 2)[:], 1024)]
-        for lane, bank in ((2, 3), (3, 0)):
-            rest.append(copy_out("dc%d" % lane, nc.scalar.copy, product(lane, SLOTS, bank)[:]))
+        def scalar_scatter(window, first, dc):
+            nc.scalar.activation(window[:].indirect(entries(first, dc.shape[1])), dc, COPY)
+
+        g01 = [sbuf("g_grouped0", [P, K], BF16, AT_QP3), sbuf("g_grouped1", [P, K], BF16, AT_QG1)]
+        g_scales = sbuf("g_scales", [P, SLOTS], U8)
+        b = []
+        for s, copy in enumerate((nc.vector.tensor_copy, nc.scalar.copy)):
+            codes = sbuf("g_codes%d" % s, [P, P], U32, AT_GC0 if s == 0 else None)
+            scales = g_scales[:, s * P : (s + 1) * P]
+            g_interleave(s, copy, g01[s][:])
+            nc.vector.quantize_mx(out=codes[:].bitcast(E5M2), scales=scales, in_=g01[s][:])
+            b.append(first_product(s, codes[:], scales))
+        g23 = sbuf("g_grouped23", [P, 2 * K], BF16, AT_QP3)
+        for s, copy in enumerate((nc.vector.tensor_copy, nc.scalar.copy)):
+            g_interleave(2 + s, copy, g23[:, s * K : (s + 1) * K])
+        w_paired = {0: w_pairs("w_paired0", nc.scalar.copy, w_first[:, 0, :], AT_QG1)}
+        dk_grouped = [sbuf("dk_grouped%d" % h, [P, 2 * K], BF16, AT_DK_LATE if h == 1 else None) for h in range(2)]
+
+        def dk_tile(s):
+            turn_words(dk_pairs(s, b[s])[:], dk_grouped[s // 2][:, s % 2 * K : (s % 2 + 1) * K], nc.scalar.copy)
+
+        w0_grouped = sbuf("w0_grouped", [P, K], BF16)
+        w1_grouped = sbuf("w1_grouped", [P, K], BF16)
+        w23_grouped = sbuf("w23_grouped", [P, 2 * K], BF16, AT_W23)
+        turn_words(w_paired[0][:], w0_grouped[:], nc.scalar.copy)
+        dk_tile(0)
+        g23_codes = sbuf("g23_codes", [P, HALF], U32, AT_GC0)
+        nc.vector.quantize_mx(out=g23_codes[:].bitcast(E5M2), scales=g_scales[:, HALF:], in_=g23[:])
+        for s in range(2, TILES):
+            b.append(first_product(s, g23_codes[:, s % 2 * P : (s % 2 + 1) * P], g_scales[:, s * P : (s + 1) * P]))
+        w_paired[1] = w_pairs("w_paired1", gpsimd_round, w_second[:, 0, :], AT_QP3 - 512)
+        w_paired[2] = w_pairs("w_paired2", gpsimd_round, w_last[:, 0, :], AT_QG3 + 512)
+        dk_tile(1)
+        w_paired[3] = w_pairs("w_paired3", nc.scalar.copy, w_last[:, 1, :], AT_QG3 - 512)
+        w_quantise(0, w0_grouped[:])
+        turn_words(w_paired[1][:], w1_grouped[:], nc.scalar.copy, 0)
+        dk_tile(2)
+        dk_tile(3)
+        quantise_dk(0, dk_grouped[0][:])
+        early_acc = product(0, 0, HALF, 0)
+        w_quantise(1, w1_grouped[:])
+        second_acc = product(1, 0, HALF, 1)
+        scalar_scatter(window_a, 0, copy_out("dc00", nc.scalar.copy, early_acc)[:])
+        turn_words(w_paired[2][:], w23_grouped[:, :K], nc.vector.tensor_copy, 2)
+        turn_words(w_paired[3][:], w23_grouped[:, K:], nc.vector.tensor_copy)
+        quantise_dk(HALF, dk_grouped[1][:])
+        late_acc = product(0, HALF, HALF, 3)
+        w_quantise(2, w23_grouped[:])
+        window_c = sbuf("window_c", [P, TOKENS], F32, AT_W23 + KB - 8 * KB)
+        window_d = sbuf("window_d", [P, TOKENS], F32, AT_W23 + KB)
+        windows = [window_a, window_b, window_c, window_d]
+        for window in windows[2:]:
+            nc.gpsimd.memset(window[:].bitcast(I32), 0)
 
         out_rows = out_0.rearrange("(p t) c -> p t c", t=LANES)
+
+        def store_lane(t):
+            nc.sync.dma_start(out_rows[:, t, :], windows[t][:])
+
+        vector_scatter(window_b, 0, copy_out("dc10", nc.vector.tensor_copy, second_acc, AT_DK_LATE)[:])
+        dc01 = copy_out("dc01", nc.scalar.copy, late_acc)
+        dc11 = copy_out("dc11", nc.scalar.copy, product(1, HALF, HALF, 2), AT_DC3)
+        dc2 = copy_out("dc2", nc.scalar.copy, product(2, 0, SLOTS, 0), AT_DC2)
+        vector_scatter(window_a, HALF, dc01[:])
+        store_lane(0)
+        scalar_scatter(window_b, HALF, dc11[:])
+        store_lane(1)
+        vector_scatter(window_c, 0, dc2[:])
+        store_lane(2)
+        dc3 = copy_out("dc3", nc.scalar.copy, product(3, 0, SLOTS, 1), AT_DC3)
+        for h in range(2):
+            scalar_scatter(window_d, h * HALF, dc3[:, h * HALF : (h + 1) * HALF])
+        store_lane(3)
+
         words_out = out_1[0].rearrange("p c l -> p (c l)").bitcast(I32)
-        y_scales = keep.tile([P, TOKENS], U8, name="y_scales", align_bytes=64)
-        spent = ["w_codes", "w_scales", "y_grouped2", "y_grouped3"]
-        y_grouped = [keep.tile([P, CHUNK, LANES], BF16, name="y_grouped%d" % c, tag=spent[c], align_bytes=64) for c in range(CHUNKS)]
-        pairs = {3: keep.tile([P, 2, CHUNK, 2], BF16, name="pairs3", tag="grad_scales", align_bytes=64)}
+        y_scales = sbuf("y_scales", [P, TOKENS], U8)
+        ranges = [
+            (0, 512, None),
+            (512, 1024, AT_DC3 + KB - 4 * KB),
+            (1024, 1280, None),
+            (1280, 1536, AT_DC2),
+            (1536, 2048, AT_DC3 + KB),
+        ]
+        pairs = [sbuf("pairs%d" % r, [P, 2, last - first, 2], BF16, at) for r, (first, last, at) in enumerate(ranges)]
+        y_grouped = [sbuf("y_grouped%d" % c, [P, CHUNK, LANES], BF16) for c in range(CHUNKS)]
 
-        def round_lane(copy, t, c, lo=0, hi=CHUNK, both=False):
-            src = windows[t % 3][:, c * CHUNK + lo : c * CHUNK + hi]
-            word = y_grouped[c][:, lo:hi, t // 2 * 2 : t // 2 * 2 + 2] if c < DIRECT else pairs[c][:, t // 2, lo:hi, :]
-            if both:
-                copy(word, src.unsqueeze(2).to_broadcast([P, hi - lo, 2]))
-            else:
-                copy(word[:, :, t % 2], src)
+        def round_lane(copy, t, r):
+            first, last, at = ranges[r]
+            copy(pairs[r][:, t // 2, :, t % 2], windows[t][:, first:last])
 
-        def merge(c, lo, hi):
-            nc.scalar.copy(
-                y_grouped[c][:, lo:hi, :].rearrange("p c t -> p (c t)").bitcast(F32).rearrange("p (c u) -> p c u", u=2),
-                pairs[c][:].rearrange("p u c e -> p (u c e)").bitcast(F32).rearrange("p (u c) -> p c u", u=2)[:, lo:hi, :],
+        def merge(copy, r):
+            first, last, at = ranges[r]
+            grouped = y_grouped[first // CHUNK][:, first % CHUNK : first % CHUNK + last - first, :]
+            copy(
+                grouped.rearrange("p c t -> p (c t)").bitcast(F32).rearrange("p (c u) -> p c u", u=2),
+                pairs[r][:].rearrange("p u c e -> p (u c e)").bitcast(F32).rearrange("p (u c) -> p c u", u=2),
             )
 
-        for t in range(LANES):
-            window = windows[t % 3]
-            scatter(window, SLOTS - rest[t].shape[1], rest[t])
-            nc.sync.dma_start(out_rows[:, t, :], window[:])
-            if t < LANES - 1:
-                for c in range(DIRECT):
-                    cut = min(max(SCALAR_DIRECT - c * CHUNK, 0), CHUNK)
-                    if cut > 0:
-                        round_lane(nc.scalar.copy, t, c, 0, cut, both=(t == 2))
-                    if cut < CHUNK:
-                        round_lane(gpsimd_round, t, c, cut, CHUNK, both=(t == 2))
-                round_lane(nc.scalar.copy, t, DIRECT, 0, CHUNK // 2)
-                round_lane(gpsimd_round, t, DIRECT, CHUNK // 2, CHUNK, both=(t == 2))
-
-        last = LANES - 1
-        for c in range(CHUNKS):
-            step = LAST_PIECE if c == CHUNKS - 1 else CHUNK
-            if c < DIRECT:
-                cut = min(max(VECTOR_LAST - c * CHUNK, 0), CHUNK)
-                if cut > 0:
-                    round_lane(nc.vector.tensor_copy, last, c, 0, cut)
-                if cut < CHUNK:
-                    round_lane(nc.scalar.copy, last, c, cut, CHUNK)
-            else:
-                round_lane(nc.scalar.copy, last, c)
-                for lo in range(0, CHUNK, step):
-                    merge(c, lo, lo + step)
-        for c in range(CHUNKS):
-            step = LAST_PIECE if c == CHUNKS - 1 else CHUNK
-            y_codes = keep.tile([P, CHUNK], U32, name="y_codes%d" % c, align_bytes=64)
-            for lo in range(0, CHUNK, step):
-                nc.vector.quantize_mx(
-                    out=y_codes[:, lo : lo + step].bitcast(E4M3), scales=y_scales[:, c * CHUNK + lo : c * CHUNK + lo + step],
-                    in_=y_grouped[c][:, lo : lo + step, :].rearrange("p c t -> p (c t)"))
+        for t in range(2):
+            for r in (0, 2):
+                round_lane(gpsimd_round, t, r)
+        for t in range(2):
+            round_lane(nc.vector.tensor_copy, t, 3)
+        for r in (0, 2, 3):
+            round_lane(nc.vector.tensor_copy, 2, r)
+        for t in range(2):
+            round_lane(nc.vector.tensor_copy, t, 1)
+        for r in (0, 2, 3):
+            round_lane(nc.vector.tensor_copy, 3, r)
+        for t in range(2):
+            round_lane(nc.vector.tensor_copy, t, 4)
+        for r in (0, 2, 3):
+            merge(nc.vector.tensor_copy, r)
+        for r in (1, 4):
+            for t in range(2, LANES):
+                round_lane(nc.scalar.copy, t, r)
+            merge(nc.scalar.copy, r)
+        for c in (0, 2, 1, 3):
+            y_codes = sbuf("y_codes%d" % c, [P, CHUNK], U32)
+            nc.vector.quantize_mx(
+                out=y_codes[:].bitcast(E4M3), scales=y_scales[:, c * CHUNK : (c + 1) * CHUNK],
+                in_=y_grouped[c][:].rearrange("p c t -> p (c t)"))
             nc.sync.dma_start(words_out[:, c * CHUNK : (c + 1) * CHUNK], y_codes[:].bitcast(I32))
         for quad in range(4):
             queue = nc.sync if quad % 2 == 0 else nc.scalar

@@ -26,6 +26,10 @@ CHUNKS = TOKENS // CHUNK
 HALF = SLOTS // 2
 TS_ROW = P - 1
 KB = 1024
+AT_Q_LAST = 50 * KB
+EARLY_COLS = 768
+VECTOR_COLS = 1216
+LAST_PIECE = 256
 
 FLOPS = 2 * 2 * 512 * 512 * 512
 
@@ -43,12 +47,11 @@ def tile_attend_gmla_c_pl_kernel(tc, qT, G, wk, ts, cf, offs, out_0, out_1, out_
                 return keep.tile(shape, dtype, name=name, align_bytes=64)
             return placed.tile(shape, dtype, name=name, offset=offset, align_bytes=64)
 
-        q_rows = qT.rearrange("(h m u) r -> h m u r", h=2, u=2)
+        q_rows = qT.rearrange("(h m u) r -> u m h r", h=2, u=2)
         w_rows = wk.rearrange("(m t) f -> m t f", t=LANES)
         g_rows = G.rearrange("(p j) i -> p j i", j=LANES)
         q_first = keep.tile([P, 2, K], F32, name="q_first")
-        q_second = [keep.tile([P, K], F32, name="q_second%d" % u) for u in range(2)]
-        q_raw = [[q_first[:, u, :] for u in range(2)], [q_second[u][:] for u in range(2)]]
+        q_second = [sbuf("q_second%d" % h, [P, 1, K], F32, AT_Q_LAST if h == 1 else None) for h in range(2)]
         w_first = keep.tile([P, 1, K], F32, name="w_first")
         w_second = keep.tile([P, 1, K], F32, name="w_second")
         w_last = keep.tile([P, 2, K], F32, name="w_last")
@@ -61,8 +64,8 @@ def tile_attend_gmla_c_pl_kernel(tc, qT, G, wk, ts, cf, offs, out_0, out_1, out_
         nc.sync.dma_start(cf_cols[:], cf.rearrange("(p t) o -> p (t o)", t=LANES))
         nc.sync.dma_start(ts_window[TS_ROW:P, :], ts[0:1, :])
         nc.sync.dma_start(offsets[:], offs)
-        for u in range(2):
-            nc.sync.dma_start(q_raw[1][u], q_rows[1, :, u, :])
+        for h in range(2):
+            nc.sync.dma_start(q_second[h][:], q_rows[1, :, h : h + 1, :])
         nc.sync.dma_start(g_raw[0][:], g_rows[:, :, :HALF])
         nc.sync.dma_start(g_raw[1][:], g_rows[:, :, HALF:])
         nc.sync.dma_start(w_first[:], w_rows[:, 0:1, :])
@@ -72,23 +75,14 @@ def tile_attend_gmla_c_pl_kernel(tc, qT, G, wk, ts, cf, offs, out_0, out_1, out_
         ident = keep.tile([P, P], F32, name="ident")
         make_identity(nc, ident[:])
 
-        def zero_one_port(part):
-            width = part.shape[1]
-            nc.vector.memset(part[:, : width - 1].bitcast(I32), 0)
-            nc.vector.memset(part[:, width - 1 :].bitcast(I32), 0)
-
-        zero_one_port(ts_window[0:TS_ROW, :])
+        nc.vector.memset(ts_window[0:TS_ROW, :].bitcast(I32), 0)
         window_a = sbuf("window_a", [P, TOKENS], F32)
-        nc.gpsimd.memset(window_a[:].bitcast(I32), 0)
-
-        ts_row = keep.tile([P, SLOTS], F32, name="ts_row")
-        nc.vector.tensor_copy(ts_row[:], ts_window[:].indirect(offsets[:]))
-
         window_b = sbuf("window_b", [P, TOKENS], F32)
-        nc.gpsimd.memset(window_b[:].bitcast(I32), 0)
+        for window in (window_a, window_b):
+            nc.vector.memset(window[:].bitcast(I32), 0)
 
         def round_pairs(round_copy, raw, order, paired):
-            round_copy(paired[:].rearrange("m (u p e) -> m u p e", u=2, e=2), raw.rearrange(order, u=2, e=2))
+            round_copy(paired.rearrange("m (u p e) -> m u p e", u=2, e=2), raw.rearrange(order, u=2, e=2))
 
         def turn_words(paired, grouped, copy, bank=None):
             words = paired.bitcast(F32)
@@ -106,46 +100,49 @@ def tile_attend_gmla_c_pl_kernel(tc, qT, G, wk, ts, cf, offs, out_0, out_1, out_
 
         cf_wide = keep.tile([P, LANES, P], F32, name="cf_wide")
         nc.scalar.copy(cf_wide[:], cf_cols[:].unsqueeze(2).to_broadcast([P, LANES, P]))
+        ts_rows = [sbuf("ts_row%d" % h, [P, HALF], F32, AT_Q_LAST if h == 1 else None) for h in range(2)]
+        nc.scalar.activation(ts_rows[0][:], ts_window[:].indirect(offsets[:, : HALF // 16]), COPY)
         cf_turned = turn.tile([P, LANES, P], F32, name="turned")
         for t in range(LANES):
             nc.tensor.transpose(cf_turned[:, t, :], cf_wide[:, t, :], ident[:])
 
-        cf_all = keep.tile([P, K], F32, name="cf_all")
+        q_codes = sbuf("q_codes", [P, K], U32)
+        q_scales = sbuf("q_scales", [P, K], U8)
+
+        AT_QP3, AT_QG3 = 1 * KB, 4 * KB
+        AT_QG0 = 46 * KB
+        AT_W23 = 6 * KB
+        AT_DK_LATE = 16 * KB
+        AT_DC20 = 28 * KB
+        AT_DC30 = 40 * KB
+
+        def q_operand(first, raw, paired_at=None, grouped_at=None):
+            count = raw.shape[1]
+            cols = slice(first * P, (first + count) * P)
+            paired = sbuf("q_paired%d" % first, [P, count * K], BF16, paired_at)
+            nc.vector.tensor_copy(
+                paired[:].rearrange("m (h u p e) -> m h u p e", h=count, u=2, e=2),
+                raw.rearrange("m h (p u e) -> m h u p e", u=2, e=2))
+            grouped = sbuf("q_grouped%d" % first, [P, count * K], BF16, grouped_at)
+            turn_words(paired[:], grouped[:], nc.scalar.copy)
+            nc.vector.quantize_mx(out=q_codes[:, cols].bitcast(E4M3), scales=q_scales[:, cols], in_=grouped[:])
+
+        q_operand(0, q_first[:], None, AT_QG0)
+        q_operand(2, q_second[0][:])
+        q_operand(3, q_second[1][:], AT_QP3, AT_QG3)
+        nc.vector.tensor_copy(ts_rows[1][:], ts_window[:].indirect(offsets[:, HALF // 16 :]))
+
+        cf_all = sbuf("cf_all", [P, K], F32, AT_QG0 + 512 - 2 * KB)
         nc.scalar.copy(
             cf_all[:].rearrange("i (u p e) -> i u p e", u=2, e=2),
             cf_turned[:].rearrange("i (e u) p -> i u p e", u=2),
         )
 
-        q_codes = sbuf("q_codes", [P, K], U32)
-        q_scales = sbuf("q_scales", [P, K], U8)
-
-        AT_QG1, AT_QP3, AT_QG3 = 0, 1 * KB, 2 * KB
-        AT_GC0 = 4 * KB
-        AT_DK_LATE = 5 * KB
-        AT_W23 = 16 * KB
-        AT_DC2 = 28 * KB
-        AT_DC3 = 40 * KB
-
-        def q_operand(h, u, round_copy):
-            t = 2 * u + h
-            cols = slice(t * P, (t + 1) * P)
-            paired = sbuf("q_paired%d" % t, [P, K], BF16, {3: AT_QP3}.get(t))
-            round_pairs(round_copy, q_raw[h][u], "m (p u e) -> m u p e", paired)
-            grouped = sbuf("q_grouped%d" % t, [P, K], BF16, {1: AT_QG1, 3: AT_QG3}.get(t))
-            turn_words(paired[:], grouped[:], nc.scalar.copy)
-            nc.vector.quantize_mx(out=q_codes[:, cols].bitcast(E4M3), scales=q_scales[:, cols], in_=grouped[:])
-
-        q_operand(0, 0, nc.scalar.copy)
-        q_operand(0, 1, nc.vector.tensor_copy)
-
-        ts_turned = turn.tile([P, TILES, P], F32, name="turned")
+        ts_turned = psum.tile([P, TILES, P], F32, name="acc3")
         for s in range(TILES):
-            nc.tensor.transpose(ts_turned[:, s, :], ts_row[:, s * P : (s + 1) * P], ident[:])
+            nc.tensor.transpose(ts_turned[:, s, :], ts_rows[s // 2][:, s % 2 * P : (s % 2 + 1) * P], ident[:])
         ts_cols = keep.tile([P, TILES], F32, name="ts_cols")
         nc.scalar.copy(ts_cols[:], ts_turned[:, :, TS_ROW])
-
-        q_operand(1, 0, nc.vector.tensor_copy)
-        q_operand(1, 1, nc.vector.tensor_copy)
 
         dk_codes = sbuf("dk_codes", [P, SLOTS], U32)
         dk_scales = sbuf("dk_scales", [P, SLOTS], U8)
@@ -155,8 +152,7 @@ def tile_attend_gmla_c_pl_kernel(tc, qT, G, wk, ts, cf, offs, out_0, out_1, out_
         def gpsimd_round(out, in_):
             nc.gpsimd.tensor_scalar(out=out, in0=in_, scalar1=1.0, scalar2=0.0, op0=MULT, op1=ADD)
 
-        def g_interleave(s, copy, grouped):
-            src = g_raw[s // 2][:, :, (s % 2) * P : (s % 2 + 1) * P]
+        def g_interleave(src, copy, grouped):
             copy(grouped.rearrange("p (c i t) -> p c t i", i=4, t=LANES), src.rearrange("p t (c i) -> p c t i", i=4))
 
         def first_product(s, codes, scales):
@@ -176,11 +172,6 @@ def tile_attend_gmla_c_pl_kernel(tc, qT, G, wk, ts, cf, offs, out_0, out_1, out_
             cols = slice(first, first + grouped.shape[1] // LANES)
             nc.vector.quantize_mx(out=dk_codes[:, cols].bitcast(E5M2), scales=dk_scales[:, cols], in_=grouped)
 
-        def w_pairs(name, round_copy, raw, offset):
-            paired = sbuf(name, [P, K], BF16, offset)
-            round_pairs(round_copy, raw, "m (p e u) -> m u p e", paired)
-            return paired
-
         def w_quantise(lane, grouped):
             cols = slice(lane * P, lane * P + grouped.shape[1] // LANES)
             nc.vector.quantize_mx(out=w_codes[:, cols].bitcast(E4M3), scales=w_scales[:, cols], in_=grouped)
@@ -196,7 +187,7 @@ def tile_attend_gmla_c_pl_kernel(tc, qT, G, wk, ts, cf, offs, out_0, out_1, out_
 
         def copy_out(name, copy, acc, offset=None):
             dc = sbuf(name, [P, acc.shape[1]], F32, offset)
-            copy(dc[:], acc[:])
+            copy(dc[:], acc)
             return dc
 
         def entries(first, count):
@@ -208,19 +199,18 @@ def tile_attend_gmla_c_pl_kernel(tc, qT, G, wk, ts, cf, offs, out_0, out_1, out_
         def scalar_scatter(window, first, dc):
             nc.scalar.activation(window[:].indirect(entries(first, dc.shape[1])), dc, COPY)
 
-        g01 = [sbuf("g_grouped0", [P, K], BF16, AT_QP3), sbuf("g_grouped1", [P, K], BF16, AT_QG1)]
         g_scales = sbuf("g_scales", [P, SLOTS], U8)
+        g01 = [sbuf("g_grouped0", [P, K], BF16, AT_QP3), sbuf("g_grouped1", [P, K], BF16, AT_QG0 + KB)]
+        g01_codes = sbuf("g01_codes", [P, HALF], U32)
         b = []
+        for s in range(2):
+            cols = slice(s * P, (s + 1) * P)
+            g_interleave(g_raw[0][:, :, cols], nc.vector.tensor_copy, g01[s][:])
+            nc.vector.quantize_mx(out=g01_codes[:, cols].bitcast(E5M2), scales=g_scales[:, cols], in_=g01[s][:])
+            b.append(first_product(s, g01_codes[:, cols], g_scales[:, cols]))
+        g23 = sbuf("g_grouped23", [P, 2 * K], BF16, AT_QG3 - KB)
         for s, copy in enumerate((nc.vector.tensor_copy, nc.scalar.copy)):
-            codes = sbuf("g_codes%d" % s, [P, P], U32, AT_GC0 if s == 0 else None)
-            scales = g_scales[:, s * P : (s + 1) * P]
-            g_interleave(s, copy, g01[s][:])
-            nc.vector.quantize_mx(out=codes[:].bitcast(E5M2), scales=scales, in_=g01[s][:])
-            b.append(first_product(s, codes[:], scales))
-        g23 = sbuf("g_grouped23", [P, 2 * K], BF16, AT_QP3)
-        for s, copy in enumerate((nc.vector.tensor_copy, nc.scalar.copy)):
-            g_interleave(2 + s, copy, g23[:, s * K : (s + 1) * K])
-        w_paired = {0: w_pairs("w_paired0", nc.scalar.copy, w_first[:, 0, :], AT_QG1)}
+            g_interleave(g_raw[1][:, :, s * P : (s + 1) * P], copy, g23[:, s * K : (s + 1) * K])
         dk_grouped = [sbuf("dk_grouped%d" % h, [P, 2 * K], BF16, AT_DK_LATE if h == 1 else None) for h in range(2)]
 
         def dk_tile(s):
@@ -229,32 +219,41 @@ def tile_attend_gmla_c_pl_kernel(tc, qT, G, wk, ts, cf, offs, out_0, out_1, out_
         w0_grouped = sbuf("w0_grouped", [P, K], BF16)
         w1_grouped = sbuf("w1_grouped", [P, K], BF16)
         w23_grouped = sbuf("w23_grouped", [P, 2 * K], BF16, AT_W23)
-        turn_words(w_paired[0][:], w0_grouped[:], nc.scalar.copy)
+        w_raw = [w_first[:, 0, :], w_second[:, 0, :], w_last[:, 0, :], w_last[:, 1, :]]
+
+        def w_pairs(t, round_copy, offset):
+            paired = sbuf("w_paired%d" % t, [P, K], BF16, offset)
+            round_pairs(round_copy, w_raw[t], "m (p e u) -> m u p e", paired[:])
+            return paired[:]
+
+        w0_paired = w_pairs(0, nc.scalar.copy, AT_QG0 + KB + 512)
+        w1_paired = w_pairs(1, nc.scalar.copy, AT_QG0 + KB + 512 - KB)
+        turn_words(w0_paired, w0_grouped[:], nc.scalar.copy)
         dk_tile(0)
-        g23_codes = sbuf("g23_codes", [P, HALF], U32, AT_GC0)
+        g23_codes = sbuf("g23_codes", [P, HALF], U32)
         nc.vector.quantize_mx(out=g23_codes[:].bitcast(E5M2), scales=g_scales[:, HALF:], in_=g23[:])
         for s in range(2, TILES):
             b.append(first_product(s, g23_codes[:, s % 2 * P : (s % 2 + 1) * P], g_scales[:, s * P : (s + 1) * P]))
-        w_paired[1] = w_pairs("w_paired1", gpsimd_round, w_second[:, 0, :], AT_QP3 - 512)
-        w_paired[2] = w_pairs("w_paired2", gpsimd_round, w_last[:, 0, :], AT_QG3 + 512)
+        w2_paired = w_pairs(2, gpsimd_round, AT_QG3 - KB)
+        w3_paired = w_pairs(3, gpsimd_round, AT_QG3)
+        turn_words(w1_paired, w1_grouped[:], nc.scalar.copy, 0)
         dk_tile(1)
-        w_paired[3] = w_pairs("w_paired3", nc.scalar.copy, w_last[:, 1, :], AT_QG3 - 512)
         w_quantise(0, w0_grouped[:])
-        turn_words(w_paired[1][:], w1_grouped[:], nc.scalar.copy, 0)
+        turn_words(w2_paired, w23_grouped[:, :K], nc.scalar.copy, 1)
         dk_tile(2)
+        turn_words(w3_paired, w23_grouped[:, K:], nc.vector.tensor_copy, 2)
         dk_tile(3)
         quantise_dk(0, dk_grouped[0][:])
         early_acc = product(0, 0, HALF, 0)
         w_quantise(1, w1_grouped[:])
         second_acc = product(1, 0, HALF, 1)
-        scalar_scatter(window_a, 0, copy_out("dc00", nc.scalar.copy, early_acc)[:])
-        turn_words(w_paired[2][:], w23_grouped[:, :K], nc.vector.tensor_copy, 2)
-        turn_words(w_paired[3][:], w23_grouped[:, K:], nc.vector.tensor_copy)
-        quantise_dk(HALF, dk_grouped[1][:])
-        late_acc = product(0, HALF, HALF, 3)
+        scalar_scatter(window_a, 0, copy_out("dc00", nc.scalar.copy, early_acc[:])[:])
         w_quantise(2, w23_grouped[:])
-        window_c = sbuf("window_c", [P, TOKENS], F32, AT_W23 + KB - 8 * KB)
-        window_d = sbuf("window_d", [P, TOKENS], F32, AT_W23 + KB)
+        dc10 = copy_out("dc10", nc.vector.tensor_copy, second_acc[:], AT_W23)
+        quantise_dk(HALF, dk_grouped[1][:])
+        late_acc = product(0, HALF, HALF, 2)
+        window_c = sbuf("window_c", [P, TOKENS], F32, AT_DK_LATE + KB - 8 * KB)
+        window_d = sbuf("window_d", [P, TOKENS], F32, AT_DK_LATE + KB)
         windows = [window_a, window_b, window_c, window_d]
         for window in windows[2:]:
             nc.gpsimd.memset(window[:].bitcast(I32), 0)
@@ -264,72 +263,68 @@ def tile_attend_gmla_c_pl_kernel(tc, qT, G, wk, ts, cf, offs, out_0, out_1, out_
         def store_lane(t):
             nc.sync.dma_start(out_rows[:, t, :], windows[t][:])
 
-        vector_scatter(window_b, 0, copy_out("dc10", nc.vector.tensor_copy, second_acc, AT_DK_LATE)[:])
-        dc01 = copy_out("dc01", nc.scalar.copy, late_acc)
-        dc11 = copy_out("dc11", nc.scalar.copy, product(1, HALF, HALF, 2), AT_DC3)
-        dc2 = copy_out("dc2", nc.scalar.copy, product(2, 0, SLOTS, 0), AT_DC2)
+        vector_scatter(window_b, 0, dc10[:])
+        dc01 = copy_out("dc01", nc.scalar.copy, late_acc[:])
+        dc11 = copy_out("dc11", nc.scalar.copy, product(1, HALF, HALF, 0)[:])
+        lane2_acc = product(2, 0, SLOTS, 3)
+        dc20 = copy_out("dc20", nc.scalar.copy, lane2_acc[:, :HALF], AT_DC20)
         vector_scatter(window_a, HALF, dc01[:])
         store_lane(0)
-        scalar_scatter(window_b, HALF, dc11[:])
+        scalar_scatter(window_c, 0, dc20[:])
+        vector_scatter(window_b, HALF, dc11[:])
         store_lane(1)
-        vector_scatter(window_c, 0, dc2[:])
+        dc21 = copy_out("dc21", nc.scalar.copy, lane2_acc[:, HALF:], AT_DC20 + 512)
+        lane3_acc = product(3, 0, SLOTS, 1)
+        dc30 = copy_out("dc30", nc.scalar.copy, lane3_acc[:, :HALF], AT_DC30)
+        dc31 = copy_out("dc31", nc.scalar.copy, lane3_acc[:, HALF:], AT_DC20 - 512)
+        scalar_scatter(window_d, 0, dc30[:])
+        vector_scatter(window_c, HALF, dc21[:])
         store_lane(2)
-        dc3 = copy_out("dc3", nc.scalar.copy, product(3, 0, SLOTS, 1), AT_DC3)
-        for h in range(2):
-            scalar_scatter(window_d, h * HALF, dc3[:, h * HALF : (h + 1) * HALF])
+        vector_scatter(window_d, HALF, dc31[:])
         store_lane(3)
 
         words_out = out_1[0].rearrange("p c l -> p (c l)").bitcast(I32)
         y_scales = sbuf("y_scales", [P, TOKENS], U8)
-        ranges = [
-            (0, 512, None),
-            (512, 1024, AT_DC3 + KB - 4 * KB),
-            (1024, 1280, None),
-            (1280, 1536, AT_DC2),
-            (1536, 2048, AT_DC3 + KB),
-        ]
+        ranges = [(0, EARLY_COLS, None), (EARLY_COLS, VECTOR_COLS, AT_DC20 + KB), (VECTOR_COLS, TOKENS, AT_DC30)]
         pairs = [sbuf("pairs%d" % r, [P, 2, last - first, 2], BF16, at) for r, (first, last, at) in enumerate(ranges)]
         y_grouped = [sbuf("y_grouped%d" % c, [P, CHUNK, LANES], BF16) for c in range(CHUNKS)]
 
-        def round_lane(copy, t, r):
+        def round_lane(copy, t, r, lo=None, hi=None):
             first, last, at = ranges[r]
-            copy(pairs[r][:, t // 2, :, t % 2], windows[t][:, first:last])
+            lo, hi = first if lo is None else lo, last if hi is None else hi
+            copy(pairs[r][:, t // 2, lo - first : hi - first, t % 2], windows[t][:, lo:hi])
 
-        def merge(copy, r):
+        def merge(copy, r, lo, hi):
             first, last, at = ranges[r]
-            grouped = y_grouped[first // CHUNK][:, first % CHUNK : first % CHUNK + last - first, :]
+            grouped = y_grouped[lo // CHUNK][:, lo % CHUNK : lo % CHUNK + hi - lo, :]
+            words = pairs[r][:].rearrange("p u c e -> p (u c e)").bitcast(F32).rearrange("p (u c) -> p c u", u=2)
             copy(
                 grouped.rearrange("p c t -> p (c t)").bitcast(F32).rearrange("p (c u) -> p c u", u=2),
-                pairs[r][:].rearrange("p u c e -> p (u c e)").bitcast(F32).rearrange("p (u c) -> p c u", u=2),
+                words[:, lo - first : hi - first, :],
             )
 
-        for t in range(2):
-            for r in (0, 2):
+        for r in range(2):
+            for t in range(2):
                 round_lane(gpsimd_round, t, r)
-        for t in range(2):
-            round_lane(nc.vector.tensor_copy, t, 3)
-        for r in (0, 2, 3):
-            round_lane(nc.vector.tensor_copy, 2, r)
-        for t in range(2):
-            round_lane(nc.vector.tensor_copy, t, 1)
-        for r in (0, 2, 3):
-            round_lane(nc.vector.tensor_copy, 3, r)
-        for t in range(2):
-            round_lane(nc.vector.tensor_copy, t, 4)
-        for r in (0, 2, 3):
-            merge(nc.vector.tensor_copy, r)
-        for r in (1, 4):
-            for t in range(2, LANES):
-                round_lane(nc.scalar.copy, t, r)
-            merge(nc.scalar.copy, r)
-        for c in (0, 2, 1, 3):
+        for t in range(3):
+            round_lane(nc.scalar.copy, t, 2)
+        for t in range(2, LANES):
+            for r in range(2):
+                round_lane(nc.vector.tensor_copy, t, r)
+        for r, lo, hi in ((0, 0, CHUNK), (0, CHUNK, EARLY_COLS), (1, EARLY_COLS, 2 * CHUNK), (1, 2 * CHUNK, VECTOR_COLS)):
+            merge(nc.vector.tensor_copy, r, lo, hi)
+        for lo, hi in ((VECTOR_COLS, 3 * CHUNK), (3 * CHUNK, TOKENS - LAST_PIECE), (TOKENS - LAST_PIECE, TOKENS)):
+            round_lane(nc.scalar.copy, 3, 2, lo, hi)
+            merge(nc.scalar.copy, 2, lo, hi)
+        for c in range(CHUNKS):
+            step = LAST_PIECE if c == CHUNKS - 1 else CHUNK
             y_codes = sbuf("y_codes%d" % c, [P, CHUNK], U32)
-            nc.vector.quantize_mx(
-                out=y_codes[:].bitcast(E4M3), scales=y_scales[:, c * CHUNK : (c + 1) * CHUNK],
-                in_=y_grouped[c][:].rearrange("p c t -> p (c t)"))
+            for lo in range(0, CHUNK, step):
+                nc.vector.quantize_mx(
+                    out=y_codes[:, lo : lo + step].bitcast(E4M3), scales=y_scales[:, c * CHUNK + lo : c * CHUNK + lo + step],
+                    in_=y_grouped[c][:, lo : lo + step, :].rearrange("p c t -> p (c t)"))
             nc.sync.dma_start(words_out[:, c * CHUNK : (c + 1) * CHUNK], y_codes[:].bitcast(I32))
         for quad in range(4):
-            queue = nc.sync if quad % 2 == 0 else nc.scalar
-            queue.dma_start(
+            nc.scalar.dma_start(
                 out_2[0, 4 * quad : 4 * quad + 4, :].bitcast(I32),
                 y_scales[32 * quad : 32 * quad + 4, :].bitcast(I32))

@@ -324,7 +324,5 @@ def tile_attend_gmla_c_pl_kernel(tc, qT, G, wk, ts, cf, offs, out_0, out_1, out_
                     out=y_codes[:, lo : lo + step].bitcast(E4M3), scales=y_scales[:, c * CHUNK + lo : c * CHUNK + lo + step],
                     in_=y_grouped[c][:, lo : lo + step, :].rearrange("p c t -> p (c t)"))
             nc.sync.dma_start(words_out[:, c * CHUNK : (c + 1) * CHUNK], y_codes[:].bitcast(I32))
-        for quad in range(4):
-            nc.scalar.dma_start(
-                out_2[0, 4 * quad : 4 * quad + 4, :].bitcast(I32),
-                y_scales[32 * quad : 32 * quad + 4, :].bitcast(I32))
+        for row in range(4):
+            nc.scalar.dma_start(out_2[0, row:16:4, :].bitcast(I32), y_scales[row:P:32, :].bitcast(I32))

@@ -27,7 +27,6 @@ HALF = SLOTS // 2
 TS_ROW = P - 1
 KB = 1024
 AT_Q_LAST = 50 * KB
-EARLY_COLS = 768
 VECTOR_COLS = 1216
 LAST_PIECE = 256
 
@@ -276,53 +275,52 @@ def tile_attend_gmla_c_pl_kernel(tc, qT, G, wk, ts, cf, offs, out_0, out_1, out_
         dc21 = copy_out("dc21", nc.scalar.copy, lane2_acc[:, HALF:], AT_DC20 + 512)
         lane3_acc = product(3, 0, SLOTS, 1)
         dc30 = copy_out("dc30", nc.scalar.copy, lane3_acc[:, :HALF], AT_DC30)
-        dc31 = copy_out("dc31", nc.scalar.copy, lane3_acc[:, HALF:], AT_DC20 - 512)
+        ranges = [(0, VECTOR_COLS), (VECTOR_COLS, TOKENS)]
+        pairs = [sbuf("pairs0", [P, 2 * VECTOR_COLS], F32)]
+        dc31 = pairs[0][:, VECTOR_COLS : VECTOR_COLS + HALF]
+        nc.scalar.copy(dc31, lane3_acc[:, HALF:])
         scalar_scatter(window_d, 0, dc30[:])
         vector_scatter(window_c, HALF, dc21[:])
         store_lane(2)
-        vector_scatter(window_d, HALF, dc31[:])
+        vector_scatter(window_d, HALF, dc31)
         store_lane(3)
+        pairs.append(sbuf("pairs1", [P, 2 * (TOKENS - VECTOR_COLS)], F32, AT_DC30))
 
         words_out = out_1[0].rearrange("p c l -> p (c l)").bitcast(I32)
         y_scales = sbuf("y_scales", [P, TOKENS], U8)
-        ranges = [(0, EARLY_COLS, None), (EARLY_COLS, VECTOR_COLS, AT_DC20 + KB), (VECTOR_COLS, TOKENS, AT_DC30)]
-        pairs = [sbuf("pairs%d" % r, [P, 2, last - first, 2], BF16, at) for r, (first, last, at) in enumerate(ranges)]
-        y_grouped = [sbuf("y_grouped%d" % c, [P, CHUNK, LANES], BF16) for c in range(CHUNKS)]
+        y_grouped = [sbuf("y_grouped%d" % c, [P, CHUNK * 2], F32) for c in range(CHUNKS)]
 
-        def round_lane(copy, t, r, lo=None, hi=None):
-            first, last, at = ranges[r]
-            lo, hi = first if lo is None else lo, last if hi is None else hi
-            copy(pairs[r][:, t // 2, lo - first : hi - first, t % 2], windows[t][:, lo:hi])
+        def round_lane(copy, t, r, lo, hi):
+            first, last = ranges[r]
+            start = t // 2 * (last - first) - first
+            halves = pairs[r][:, start + lo : start + hi].bitcast(BF16).rearrange("p (c e) -> p c e", e=2)
+            copy(halves[:, :, t % 2], windows[t][:, lo:hi])
 
         def merge(copy, r, lo, hi):
-            first, last, at = ranges[r]
-            grouped = y_grouped[lo // CHUNK][:, lo % CHUNK : lo % CHUNK + hi - lo, :]
-            words = pairs[r][:].rearrange("p u c e -> p (u c e)").bitcast(F32).rearrange("p (u c) -> p c u", u=2)
+            first, last = ranges[r]
+            grouped = y_grouped[lo // CHUNK][:, lo % CHUNK * 2 : (lo % CHUNK + hi - lo) * 2]
             copy(
-                grouped.rearrange("p c t -> p (c t)").bitcast(F32).rearrange("p (c u) -> p c u", u=2),
-                words[:, lo - first : hi - first, :],
-            )
+                grouped.rearrange("p (c u) -> p c u", u=2),
+                pairs[r][:].rearrange("p (u c) -> p c u", u=2)[:, lo - first : hi - first, :])
 
-        for r in range(2):
-            for t in range(2):
-                round_lane(gpsimd_round, t, r)
+        for t in range(2):
+            round_lane(gpsimd_round, t, 0, 0, VECTOR_COLS)
         for t in range(3):
-            round_lane(nc.scalar.copy, t, 2)
+            round_lane(nc.scalar.copy, t, 1, VECTOR_COLS, TOKENS)
         for t in range(2, LANES):
-            for r in range(2):
-                round_lane(nc.vector.tensor_copy, t, r)
-        for r, lo, hi in ((0, 0, CHUNK), (0, CHUNK, EARLY_COLS), (1, EARLY_COLS, 2 * CHUNK), (1, 2 * CHUNK, VECTOR_COLS)):
-            merge(nc.vector.tensor_copy, r, lo, hi)
+            round_lane(nc.vector.tensor_copy, t, 0, 0, VECTOR_COLS)
+        for lo, hi in ((0, CHUNK), (CHUNK, 2 * CHUNK), (2 * CHUNK, VECTOR_COLS)):
+            merge(nc.vector.tensor_copy, 0, lo, hi)
         for lo, hi in ((VECTOR_COLS, 3 * CHUNK), (3 * CHUNK, TOKENS - LAST_PIECE), (TOKENS - LAST_PIECE, TOKENS)):
-            round_lane(nc.scalar.copy, 3, 2, lo, hi)
-            merge(nc.scalar.copy, 2, lo, hi)
+            round_lane(nc.scalar.copy, 3, 1, lo, hi)
+            merge(nc.scalar.copy, 1, lo, hi)
         for c in range(CHUNKS):
             step = LAST_PIECE if c == CHUNKS - 1 else CHUNK
             y_codes = sbuf("y_codes%d" % c, [P, CHUNK], U32)
             for lo in range(0, CHUNK, step):
                 nc.vector.quantize_mx(
                     out=y_codes[:, lo : lo + step].bitcast(E4M3), scales=y_scales[:, c * CHUNK + lo : c * CHUNK + lo + step],
-                    in_=y_grouped[c][:, lo : lo + step, :].rearrange("p c t -> p (c t)"))
+                    in_=y_grouped[c][:, 2 * lo : 2 * (lo + step)].bitcast(BF16))
             nc.sync.dma_start(words_out[:, c * CHUNK : (c + 1) * CHUNK], y_codes[:].bitcast(I32))
         for row in range(4):
             nc.scalar.dma_start(out_2[0, row:16:4, :].bitcast(I32), y_scales[row:P:32, :].bitcast(I32))

@@ -74,11 +74,11 @@ def tile_attend_gmla_c_pl_kernel(tc, qT, G, wk, ts, cf, offs, out_0, out_1, out_
         ident = keep.tile([P, P], F32, name="ident")
         make_identity(nc, ident[:])
 
-        nc.vector.memset(ts_window[0:TS_ROW, :].bitcast(I32), 0)
+        nc.vector.memset(ts_window[0:TS_ROW, 0:2048].bitcast(I32), 0)
         window_a = sbuf("window_a", [P, TOKENS], F32)
         window_b = sbuf("window_b", [P, TOKENS], F32)
-        for window in (window_a, window_b):
-            nc.vector.memset(window[:].bitcast(I32), 0)
+        nc.vector.memset(window_a[:, 0:2048].bitcast(I32), 0)
+        nc.vector.memset(window_b[:, 0:2048].bitcast(I32), 0)
 
         def round_pairs(round_copy, raw, order, paired):
             round_copy(paired.rearrange("m (u p e) -> m u p e", u=2, e=2), raw.rearrange(order, u=2, e=2))
@@ -314,13 +314,14 @@ def tile_attend_gmla_c_pl_kernel(tc, qT, G, wk, ts, cf, offs, out_0, out_1, out_
         for lo, hi in ((VECTOR_COLS, 3 * CHUNK), (3 * CHUNK, TOKENS - LAST_PIECE), (TOKENS - LAST_PIECE, TOKENS)):
             round_lane(nc.scalar.copy, 3, 1, lo, hi)
             merge(nc.scalar.copy, 1, lo, hi)
-        for c in range(CHUNKS):
-            step = LAST_PIECE if c == CHUNKS - 1 else CHUNK
-            y_codes = sbuf("y_codes%d" % c, [P, CHUNK], U32)
-            for lo in range(0, CHUNK, step):
+        pieces = [(0, CHUNK), (CHUNK, 2 * CHUNK), (2 * CHUNK, 3 * CHUNK), (3 * CHUNK, TOKENS - LAST_PIECE), (TOKENS - LAST_PIECE, TOKENS)]
+        for store in (pieces[:2], pieces[2:3], pieces[3:]):
+            first, last = store[0][0], store[-1][1]
+            y_codes = sbuf("y_codes%d" % first, [P, last - first], U32)
+            for lo, hi in store:
                 nc.vector.quantize_mx(
-                    out=y_codes[:, lo : lo + step].bitcast(E4M3), scales=y_scales[:, c * CHUNK + lo : c * CHUNK + lo + step],
-                    in_=y_grouped[c][:, 2 * lo : 2 * (lo + step)].bitcast(BF16))
-            nc.sync.dma_start(words_out[:, c * CHUNK : (c + 1) * CHUNK], y_codes[:].bitcast(I32))
+                    out=y_codes[:, lo - first : hi - first].bitcast(E4M3), scales=y_scales[:, lo:hi],
+                    in_=y_grouped[lo // CHUNK][:, lo % CHUNK * 2 : (lo % CHUNK + hi - lo) * 2].bitcast(BF16))
+            nc.sync.dma_start(words_out[:, first:last], y_codes[:].bitcast(I32))
         for row in range(4):
             nc.scalar.dma_start(out_2[0, row:16:4, :].bitcast(I32), y_scales[row:P:32, :].bitcast(I32))

@@ -277,7 +277,7 @@ def tile_attend_gmla_c_pl_kernel(tc, qT, G, wk, ts, cf, offs, out_0, out_1, out_
         dc30 = copy_out("dc30", nc.scalar.copy, lane3_acc[:, :HALF], AT_DC30)
         ranges = [(0, VECTOR_COLS), (VECTOR_COLS, TOKENS)]
         pairs = [sbuf("pairs0", [P, 2 * VECTOR_COLS], F32)]
-        dc31 = pairs[0][:, VECTOR_COLS : VECTOR_COLS + HALF]
+        dc31 = pairs[0][:, VECTOR_COLS + 2 * CHUNK - P : VECTOR_COLS + 2 * CHUNK + P]
         nc.scalar.copy(dc31, lane3_acc[:, HALF:])
         scalar_scatter(window_d, 0, dc30[:])
         vector_scatter(window_c, HALF, dc21[:])
@@ -307,21 +307,32 @@ def tile_attend_gmla_c_pl_kernel(tc, qT, G, wk, ts, cf, offs, out_0, out_1, out_
             round_lane(gpsimd_round, t, 0, 0, VECTOR_COLS)
         for t in range(3):
             round_lane(nc.scalar.copy, t, 1, VECTOR_COLS, TOKENS)
-        for t in range(2, LANES):
-            round_lane(nc.vector.tensor_copy, t, 0, 0, VECTOR_COLS)
-        for lo, hi in ((0, CHUNK), (CHUNK, 2 * CHUNK), (2 * CHUNK, VECTOR_COLS)):
-            merge(nc.vector.tensor_copy, 0, lo, hi)
         for lo, hi in ((VECTOR_COLS, 3 * CHUNK), (3 * CHUNK, TOKENS - LAST_PIECE), (TOKENS - LAST_PIECE, TOKENS)):
             round_lane(nc.scalar.copy, 3, 1, lo, hi)
             merge(nc.scalar.copy, 1, lo, hi)
-        pieces = [(0, CHUNK), (CHUNK, 2 * CHUNK), (2 * CHUNK, 3 * CHUNK), (3 * CHUNK, TOKENS - LAST_PIECE), (TOKENS - LAST_PIECE, TOKENS)]
-        for store in (pieces[:2], pieces[2:3], pieces[3:]):
-            first, last = store[0][0], store[-1][1]
-            y_codes = sbuf("y_codes%d" % first, [P, last - first], U32)
-            for lo, hi in store:
-                nc.vector.quantize_mx(
-                    out=y_codes[:, lo - first : hi - first].bitcast(E4M3), scales=y_scales[:, lo:hi],
-                    in_=y_grouped[lo // CHUNK][:, lo % CHUNK * 2 : (lo % CHUNK + hi - lo) * 2].bitcast(BF16))
-            nc.sync.dma_start(words_out[:, first:last], y_codes[:].bitcast(I32))
+
+        stores = [(0, 2 * CHUNK), (2 * CHUNK, 3 * CHUNK), (3 * CHUNK, TOKENS)]
+        y_codes = [sbuf("y_codes%d" % lo, [P, hi - lo], U32) for lo, hi in stores]
+
+        def planes(store, lo, hi):
+            first, last = stores[store]
+            nc.vector.quantize_mx(
+                out=y_codes[store][:, lo - first : hi - first].bitcast(E4M3), scales=y_scales[:, lo:hi],
+                in_=y_grouped[lo // CHUNK][:, lo % CHUNK * 2 : (lo % CHUNK + hi - lo) * 2].bitcast(BF16))
+            if hi == last:
+                nc.sync.dma_start(words_out[:, first:last], y_codes[store][:].bitcast(I32))
+
+        for t in range(2, LANES):
+            round_lane(nc.vector.tensor_copy, t, 0, 0, 2 * CHUNK)
+        merge(nc.vector.tensor_copy, 0, 0, CHUNK)
+        merge(nc.vector.tensor_copy, 0, CHUNK, 2 * CHUNK)
+        planes(0, 0, CHUNK)
+        planes(0, CHUNK, 2 * CHUNK)
+        for t in range(2, LANES):
+            round_lane(nc.vector.tensor_copy, t, 0, 2 * CHUNK, VECTOR_COLS)
+        merge(nc.vector.tensor_copy, 0, 2 * CHUNK, VECTOR_COLS)
+        planes(1, 2 * CHUNK, 3 * CHUNK)
+        planes(2, 3 * CHUNK, TOKENS - LAST_PIECE)
+        planes(2, TOKENS - LAST_PIECE, TOKENS)
         for row in range(4):
             nc.scalar.dma_start(out_2[0, row:16:4, :].bitcast(I32), y_scales[row:P:32, :].bitcast(I32))

@@ -76,9 +76,7 @@ def tile_attend_gmla_c_pl_kernel(tc, qT, G, wk, ts, cf, offs, out_0, out_1, out_
 
         nc.vector.memset(ts_window[0:TS_ROW, 0:2048].bitcast(I32), 0)
         window_a = sbuf("window_a", [P, TOKENS], F32)
-        window_b = sbuf("window_b", [P, TOKENS], F32)
         nc.vector.memset(window_a[:, 0:2048].bitcast(I32), 0)
-        nc.vector.memset(window_b[:, 0:2048].bitcast(I32), 0)
 
         def round_pairs(round_copy, raw, order, paired):
             round_copy(paired.rearrange("m (u p e) -> m u p e", u=2, e=2), raw.rearrange(order, u=2, e=2))
@@ -130,6 +128,9 @@ def tile_attend_gmla_c_pl_kernel(tc, qT, G, wk, ts, cf, offs, out_0, out_1, out_
         q_operand(2, q_second[0][:])
         q_operand(3, q_second[1][:], AT_QP3, AT_QG3)
         nc.vector.tensor_copy(ts_rows[1][:], ts_window[:].indirect(offsets[:, HALF // 16 :]))
+        window_b = sbuf("window_b", [P, TOKENS], F32, AT_Q_LAST + KB)
+        nc.gpsimd.memset(window_b[:, :CHUNK].bitcast(I32), 0)
+        nc.vector.memset(window_b[:, CHUNK:].bitcast(I32), 0)
 
         cf_all = sbuf("cf_all", [P, K], F32, AT_QG0 + 512 - 2 * KB)
         nc.scalar.copy(

@@ -76,7 +76,9 @@ def tile_attend_gmla_c_pl_kernel(tc, qT, G, wk, ts, cf, offs, out_0, out_1, out_
 
         nc.vector.memset(ts_window[0:TS_ROW, 0:2048].bitcast(I32), 0)
         window_a = sbuf("window_a", [P, TOKENS], F32)
+        window_b = sbuf("window_b", [P, TOKENS], F32)
         nc.vector.memset(window_a[:, 0:2048].bitcast(I32), 0)
+        nc.vector.memset(window_b[:, 0:1024].bitcast(I32), 0)
 
         def round_pairs(round_copy, raw, order, paired):
             round_copy(paired.rearrange("m (u p e) -> m u p e", u=2, e=2), raw.rearrange(order, u=2, e=2))
@@ -128,9 +130,7 @@ def tile_attend_gmla_c_pl_kernel(tc, qT, G, wk, ts, cf, offs, out_0, out_1, out_
         q_operand(2, q_second[0][:])
         q_operand(3, q_second[1][:], AT_QP3, AT_QG3)
         nc.vector.tensor_copy(ts_rows[1][:], ts_window[:].indirect(offsets[:, HALF // 16 :]))
-        window_b = sbuf("window_b", [P, TOKENS], F32, AT_Q_LAST + KB)
-        nc.gpsimd.memset(window_b[:, :CHUNK].bitcast(I32), 0)
-        nc.vector.memset(window_b[:, CHUNK:].bitcast(I32), 0)
+        nc.vector.memset(window_b[:, 1024:2048].bitcast(I32), 0)
 
         cf_all = sbuf("cf_all", [P, K], F32, AT_QG0 + 512 - 2 * KB)
         nc.scalar.copy(

from contextlib import ExitStack

import concourse.mybir as mybir
from concourse.masks import make_identity

F32 = mybir.dt.float32
BF16 = mybir.dt.bfloat16
I32 = mybir.dt.int32
U32 = mybir.dt.uint32
U16 = mybir.dt.uint16
U8 = mybir.dt.uint8
E4M3 = mybir.dt.float8_e4m3fn_x4
E5M2 = mybir.dt.float8_e5m2_x4
MULT = mybir.AluOpType.mult
ADD = mybir.AluOpType.add
COPY = mybir.ActivationFunctionType.Copy

P = 128
LANES = 4
K = 512
SLOTS = 512
TILES = SLOTS // P
TOKENS = 2048
CHUNK = 512
CHUNKS = TOKENS // CHUNK
HALF = SLOTS // 2
TS_ROW = P - 1
KB = 1024
AT_Q_LAST = 50 * KB
VECTOR_COLS = 1216
LAST_PIECE = 256

FLOPS = 2 * 2 * 512 * 512 * 512


def tile_attend_gmla_c_pl_kernel(tc, qT, G, wk, ts, cf, offs, out_0, out_1, out_2):
    nc = tc.nc
    with ExitStack() as ctx:
        keep = ctx.enter_context(tc.tile_pool(name="keep", bufs=1))
        psum = ctx.enter_context(tc.psum_pool(name="psum", bufs=1))
        turn = ctx.enter_context(tc.psum_pool(name="turn", bufs=4))
        placed = ctx.enter_context(tc.tile_pool(name="placed", bufs=1))

        def sbuf(name, shape, dtype, offset=None):
            if offset is None:
                return keep.tile(shape, dtype, name=name, align_bytes=64)
            return placed.tile(shape, dtype, name=name, offset=offset, align_bytes=64)

        q_rows = qT.rearrange("(h m u) r -> u m h r", h=2, u=2)
        w_rows = wk.rearrange("(m t) f -> m t f", t=LANES)
        g_rows = G.rearrange("(p j) i -> p j i", j=LANES)
        q_first = keep.tile([P, 2, K], F32, name="q_first")
        q_second = [sbuf("q_second%d" % h, [P, 1, K], F32, AT_Q_LAST if h == 1 else None) for h in range(2)]
        w_first = keep.tile([P, 1, K], F32, name="w_first")
        w_second = keep.tile([P, 1, K], F32, name="w_second")
        w_last = keep.tile([P, 2, K], F32, name="w_last")
        g_raw = [keep.tile([P, LANES, HALF], F32, name="g_raw%d" % h) for h in range(2)]
        offsets = keep.tile([P, SLOTS // 16], U16, name="offsets")
        ts_window = keep.tile([P, TOKENS], F32, name="ts_window")
        cf_cols = keep.tile([P, LANES], F32, name="cf_cols")

        nc.scalar.dma_start(q_first[:], q_rows[0])
        nc.sync.dma_start(cf_cols[:], cf.rearrange("(p t) o -> p (t o)", t=LANES))
        nc.sync.dma_start(ts_window[TS_ROW:P, :], ts[0:1, :])
        nc.sync.dma_start(offsets[:], offs)
        for h in range(2):
            nc.sync.dma_start(q_second[h][:], q_rows[1, :, h : h + 1, :])
        nc.sync.dma_start(g_raw[0][:], g_rows[:, :, :HALF])
        nc.sync.dma_start(g_raw[1][:], g_rows[:, :, HALF:])
        nc.sync.dma_start(w_first[:], w_rows[:, 0:1, :])
        nc.sync.dma_start(w_second[:], w_rows[:, 1:2, :])
        nc.sync.dma_start(w_last[:], w_rows[:, 2:, :])

        ident = keep.tile([P, P], F32, name="ident")
        make_identity(nc, ident[:])

        nc.vector.memset(ts_window[0:TS_ROW, 0:2048].bitcast(I32), 0)
        window_a = sbuf("window_a", [P, TOKENS], F32)
        window_b = sbuf("window_b", [P, TOKENS], F32)
        nc.vector.memset(window_a[:, 0:2048].bitcast(I32), 0)
        nc.vector.memset(window_b[:, 0:1024].bitcast(I32), 0)

        def round_pairs(round_copy, raw, order, paired):
            round_copy(paired.rearrange("m (u p e) -> m u p e", u=2, e=2), raw.rearrange(order, u=2, e=2))

        def turn_words(paired, grouped, copy, bank=None):
            words = paired.bitcast(F32)
            blocks = words.shape[1] // P
            if bank is None:
                turned = turn.tile([P, blocks, P], F32, name="turned")
            else:
                turned = psum.tile([P, blocks, P], F32, name="acc%d" % bank)
            for block in range(blocks):
                nc.tensor.transpose(turned[:, block, :], words[:, block * P : (block + 1) * P], ident[:])
            copy(
                grouped.bitcast(F32).rearrange("p (t m u) -> p t m u", m=P, u=2),
                turned[:].rearrange("p (t u) m -> p t m u", u=2),
            )

        cf_wide = keep.tile([P, LANES, P], F32, name="cf_wide")
        nc.scalar.copy(cf_wide[:], cf_cols[:].unsqueeze(2).to_broadcast([P, LANES, P]))
        ts_rows = [sbuf("ts_row%d" % h, [P, HALF], F32, AT_Q_LAST if h == 1 else None) for h in range(2)]
        nc.scalar.activation(ts_rows[0][:], ts_window[:].indirect(offsets[:, : HALF // 16]), COPY)
        cf_turned = turn.tile([P, LANES, P], F32, name="turned")
        for t in range(LANES):
            nc.tensor.transpose(cf_turned[:, t, :], cf_wide[:, t, :], ident[:])

        q_codes = sbuf("q_codes", [P, K], U32)
        q_scales = sbuf("q_scales", [P, K], U8)

        AT_QP3, AT_QG3 = 1 * KB, 4 * KB
        AT_QG0 = 46 * KB
        AT_W23 = 6 * KB
        AT_DK_LATE = 16 * KB
        AT_DC20 = 28 * KB
        AT_DC30 = 40 * KB

        def q_operand(first, raw, paired_at=None, grouped_at=None):
            count = raw.shape[1]
            cols = slice(first * P, (first + count) * P)
            paired = sbuf("q_paired%d" % first, [P, count * K], BF16, paired_at)
            nc.vector.tensor_copy(
                paired[:].rearrange("m (h u p e) -> m h u p e", h=count, u=2, e=2),
                raw.rearrange("m h (p u e) -> m h u p e", u=2, e=2))
            grouped = sbuf("q_grouped%d" % first, [P, count * K], BF16, grouped_at)
            turn_words(paired[:], grouped[:], nc.scalar.copy)
            nc.vector.quantize_mx(out=q_codes[:, cols].bitcast(E4M3), scales=q_scales[:, cols], in_=grouped[:])

        q_operand(0, q_first[:], None, AT_QG0)
        q_operand(2, q_second[0][:])
        q_operand(3, q_second[1][:], AT_QP3, AT_QG3)
        nc.vector.tensor_copy(ts_rows[1][:], ts_window[:].indirect(offsets[:, HALF // 16 :]))
        nc.vector.memset(window_b[:, 1024:2048].bitcast(I32), 0)

        cf_all = sbuf("cf_all", [P, K], F32, AT_QG0 + 512 - 2 * KB)
        nc.scalar.copy(
            cf_all[:].rearrange("i (u p e) -> i u p e", u=2, e=2),
            cf_turned[:].rearrange("i (e u) p -> i u p e", u=2),
        )

        ts_turned = psum.tile([P, TILES, P], F32, name="acc3")
        for s in range(TILES):
            nc.tensor.transpose(ts_turned[:, s, :], ts_rows[s // 2][:, s % 2 * P : (s % 2 + 1) * P], ident[:])
        ts_cols = keep.tile([P, TILES], F32, name="ts_cols")
        nc.scalar.copy(ts_cols[:], ts_turned[:, :, TS_ROW])

        dk_codes = sbuf("dk_codes", [P, SLOTS], U32)
        dk_scales = sbuf("dk_scales", [P, SLOTS], U8)
        w_codes = sbuf("w_codes", [P, K], U32)
        w_scales = sbuf("w_scales", [P, K], U8)

        def gpsimd_round(out, in_):
            nc.gpsimd.tensor_scalar(out=out, in0=in_, scalar1=1.0, scalar2=0.0, op0=MULT, op1=ADD)

        def g_interleave(src, copy, grouped):
            copy(grouped.rearrange("p (c i t) -> p c t i", i=4, t=LANES), src.rearrange("p t (c i) -> p c t i", i=4))

        def first_product(s, codes, scales):
            acc = psum.tile([P, K], F32, name="acc%d" % s)
            nc.tensor.matmul_mx(
                out=acc[:], lhsT=codes.bitcast(E5M2), lhsT_scale=scales,
                rhs=q_codes[:].bitcast(E4M3), rhs_scale=q_scales[:], start=True, stop=True)
            return acc

        def dk_pairs(s, acc):
            paired = sbuf("dk_paired%d" % s, [P, K], BF16)
            nc.vector.scalar_tensor_tensor(
                out=paired[:], in0=acc[:], scalar=ts_cols[:, s : s + 1], in1=cf_all[:], op0=MULT, op1=MULT)
            return paired

        def quantise_dk(first, grouped):
            cols = slice(first, first + grouped.shape[1] // LANES)
            nc.vector.quantize_mx(out=dk_codes[:, cols].bitcast(E5M2), scales=dk_scales[:, cols], in_=grouped)

        def w_quantise(lane, grouped):
            cols = slice(lane * P, lane * P + grouped.shape[1] // LANES)
            nc.vector.quantize_mx(out=w_codes[:, cols].bitcast(E4M3), scales=w_scales[:, cols], in_=grouped)

        def product(lane, first, count, bank):
            cols = slice(lane * P, (lane + 1) * P)
            moving = slice(first, first + count)
            acc = psum.tile([P, count], F32, name="acc%d" % bank)
            nc.tensor.matmul_mx(
                out=acc[:], lhsT=w_codes[:, cols].bitcast(E4M3), lhsT_scale=w_scales[:, cols],
                rhs=dk_codes[:, moving].bitcast(E5M2), rhs_scale=dk_scales[:, moving], start=True, stop=True)
            return acc

        def copy_out(name, copy, acc, offset=None):
            dc = sbuf(name, [P, acc.shape[1]], F32, offset)
            copy(dc[:], acc)
            return dc

        def entries(first, count):
            return offsets[:, first // 16 : (first + count) // 16]

        def vector_scatter(window, first, dc):
            nc.vector.tensor_copy(window[:].indirect(entries(first, dc.shape[1])), dc)

        def scalar_scatter(window, first, dc):
            nc.scalar.activation(window[:].indirect(entries(first, dc.shape[1])), dc, COPY)

        g_scales = sbuf("g_scales", [P, SLOTS], U8)
        g01 = [sbuf("g_grouped0", [P, K], BF16, AT_QP3), sbuf("g_grouped1", [P, K], BF16, AT_QG0 + KB)]
        g01_codes = sbuf("g01_codes", [P, HALF], U32)
        b = []
        for s in range(2):
            cols = slice(s * P, (s + 1) * P)
            g_interleave(g_raw[0][:, :, cols], nc.vector.tensor_copy, g01[s][:])
            nc.vector.quantize_mx(out=g01_codes[:, cols].bitcast(E5M2), scales=g_scales[:, cols], in_=g01[s][:])
            b.append(first_product(s, g01_codes[:, cols], g_scales[:, cols]))
        g23 = sbuf("g_grouped23", [P, 2 * K], BF16, AT_QG3 - KB)
        for s, copy in enumerate((nc.vector.tensor_copy, nc.scalar.copy)):
            g_interleave(g_raw[1][:, :, s * P : (s + 1) * P], copy, g23[:, s * K : (s + 1) * K])
        dk_grouped = [sbuf("dk_grouped%d" % h, [P, 2 * K], BF16, AT_DK_LATE if h == 1 else None) for h in range(2)]

        def dk_tile(s):
            turn_words(dk_pairs(s, b[s])[:], dk_grouped[s // 2][:, s % 2 * K : (s % 2 + 1) * K], nc.scalar.copy)

        w0_grouped = sbuf("w0_grouped", [P, K], BF16)
        w1_grouped = sbuf("w1_grouped", [P, K], BF16)
        w23_grouped = sbuf("w23_grouped", [P, 2 * K], BF16, AT_W23)
        w_raw = [w_first[:, 0, :], w_second[:, 0, :], w_last[:, 0, :], w_last[:, 1, :]]

        def w_pairs(t, round_copy, offset):
            paired = sbuf("w_paired%d" % t, [P, K], BF16, offset)
            round_pairs(round_copy, w_raw[t], "m (p e u) -> m u p e", paired[:])
            return paired[:]

        w0_paired = w_pairs(0, nc.scalar.copy, AT_QG0 + KB + 512)
        w1_paired = w_pairs(1, nc.scalar.copy, AT_QG0 + KB + 512 - KB)
        turn_words(w0_paired, w0_grouped[:], nc.scalar.copy)
        dk_tile(0)
        g23_codes = sbuf("g23_codes", [P, HALF], U32)
        nc.vector.quantize_mx(out=g23_codes[:].bitcast(E5M2), scales=g_scales[:, HALF:], in_=g23[:])
        for s in range(2, TILES):
            b.append(first_product(s, g23_codes[:, s % 2 * P : (s % 2 + 1) * P], g_scales[:, s * P : (s + 1) * P]))
        w2_paired = w_pairs(2, gpsimd_round, AT_QG3 - KB)
        w3_paired = w_pairs(3, gpsimd_round, AT_QG3)
        turn_words(w1_paired, w1_grouped[:], nc.scalar.copy, 0)
        dk_tile(1)
        w_quantise(0, w0_grouped[:])
        turn_words(w2_paired, w23_grouped[:, :K], nc.scalar.copy, 1)
        dk_tile(2)
        turn_words(w3_paired, w23_grouped[:, K:], nc.vector.tensor_copy, 2)
        dk_tile(3)
        quantise_dk(0, dk_grouped[0][:])
        early_acc = product(0, 0, HALF, 0)
        w_quantise(1, w1_grouped[:])
        second_acc = product(1, 0, HALF, 1)
        scalar_scatter(window_a, 0, copy_out("dc00", nc.scalar.copy, early_acc[:])[:])
        w_quantise(2, w23_grouped[:])
        dc10 = copy_out("dc10", nc.vector.tensor_copy, second_acc[:], AT_W23)
        quantise_dk(HALF, dk_grouped[1][:])
        late_acc = product(0, HALF, HALF, 2)
        window_c = sbuf("window_c", [P, TOKENS], F32, AT_DK_LATE + KB - 8 * KB)
        window_d = sbuf("window_d", [P, TOKENS], F32, AT_DK_LATE + KB)
        windows = [window_a, window_b, window_c, window_d]
        for window in windows[2:]:
            nc.gpsimd.memset(window[:].bitcast(I32), 0)

        out_rows = out_0.rearrange("(p t) c -> p t c", t=LANES)

        def store_lane(t):
            nc.sync.dma_start(out_rows[:, t, :], windows[t][:])

        vector_scatter(window_b, 0, dc10[:])
        dc01 = copy_out("dc01", nc.scalar.copy, late_acc[:])
        dc11 = copy_out("dc11", nc.scalar.copy, product(1, HALF, HALF, 0)[:])
        lane2_acc = product(2, 0, SLOTS, 3)
        dc20 = copy_out("dc20", nc.scalar.copy, lane2_acc[:, :HALF], AT_DC20)
        vector_scatter(window_a, HALF, dc01[:])
        store_lane(0)
        scalar_scatter(window_c, 0, dc20[:])
        vector_scatter(window_b, HALF, dc11[:])
        store_lane(1)
        dc21 = copy_out("dc21", nc.scalar.copy, lane2_acc[:, HALF:], AT_DC20 + 512)
        lane3_acc = product(3, 0, SLOTS, 1)
        dc30 = copy_out("dc30", nc.scalar.copy, lane3_acc[:, :HALF], AT_DC30)
        ranges = [(0, VECTOR_COLS), (VECTOR_COLS, TOKENS)]
        pairs = [sbuf("pairs0", [P, 2 * VECTOR_COLS], F32)]
        dc31 = pairs[0][:, VECTOR_COLS + 2 * CHUNK - P : VECTOR_COLS + 2 * CHUNK + P]
        nc.scalar.copy(dc31, lane3_acc[:, HALF:])
        scalar_scatter(window_d, 0, dc30[:])
        vector_scatter(window_c, HALF, dc21[:])
        store_lane(2)
        vector_scatter(window_d, HALF, dc31)
        store_lane(3)
        pairs.append(sbuf("pairs1", [P, 2 * (TOKENS - VECTOR_COLS)], F32, AT_DC30))

        words_out = out_1[0].rearrange("p c l -> p (c l)").bitcast(I32)
        y_scales = sbuf("y_scales", [P, TOKENS], U8)
        y_grouped = [sbuf("y_grouped%d" % c, [P, CHUNK * 2], F32) for c in range(CHUNKS)]

        def round_lane(copy, t, r, lo, hi):
            first, last = ranges[r]
            start = t // 2 * (last - first) - first
            halves = pairs[r][:, start + lo : start + hi].bitcast(BF16).rearrange("p (c e) -> p c e", e=2)
            copy(halves[:, :, t % 2], windows[t][:, lo:hi])

        def merge(copy, r, lo, hi):
            first, last = ranges[r]
            grouped = y_grouped[lo // CHUNK][:, lo % CHUNK * 2 : (lo % CHUNK + hi - lo) * 2]
            copy(
                grouped.rearrange("p (c u) -> p c u", u=2),
                pairs[r][:].rearrange("p (u c) -> p c u", u=2)[:, lo - first : hi - first, :])

        for t in range(2):
            round_lane(gpsimd_round, t, 0, 0, VECTOR_COLS)
        for t in range(3):
            round_lane(nc.scalar.copy, t, 1, VECTOR_COLS, TOKENS)
        for lo, hi in ((VECTOR_COLS, 3 * CHUNK), (3 * CHUNK, TOKENS - LAST_PIECE), (TOKENS - LAST_PIECE, TOKENS)):
            round_lane(nc.scalar.copy, 3, 1, lo, hi)
            merge(nc.scalar.copy, 1, lo, hi)

        stores = [(0, 2 * CHUNK), (2 * CHUNK, 3 * CHUNK), (3 * CHUNK, TOKENS)]
        y_codes = [sbuf("y_codes%d" % lo, [P, hi - lo], U32) for lo, hi in stores]

        def planes(store, lo, hi):
            first, last = stores[store]
            nc.vector.quantize_mx(
                out=y_codes[store][:, lo - first : hi - first].bitcast(E4M3), scales=y_scales[:, lo:hi],
                in_=y_grouped[lo // CHUNK][:, lo % CHUNK * 2 : (lo % CHUNK + hi - lo) * 2].bitcast(BF16))
            if hi == last:
                nc.sync.dma_start(words_out[:, first:last], y_codes[store][:].bitcast(I32))

        for t in range(2, LANES):
            round_lane(nc.vector.tensor_copy, t, 0, 0, 2 * CHUNK)
        merge(nc.vector.tensor_copy, 0, 0, CHUNK)
        merge(nc.vector.tensor_copy, 0, CHUNK, 2 * CHUNK)
        planes(0, 0, CHUNK)
        planes(0, CHUNK, 2 * CHUNK)
        for t in range(2, LANES):
            round_lane(nc.vector.tensor_copy, t, 0, 2 * CHUNK, VECTOR_COLS)
        merge(nc.vector.tensor_copy, 0, 2 * CHUNK, VECTOR_COLS)
        planes(1, 2 * CHUNK, 3 * CHUNK)
        planes(2, 3 * CHUNK, TOKENS - LAST_PIECE)
        planes(2, TOKENS - LAST_PIECE, TOKENS)
        for row in range(4):
            nc.scalar.dma_start(out_2[0, row:16:4, :].bitcast(I32), y_scales[row:P:32, :].bitcast(I32))
